import numpy as np, ml_dtypes
CORES = [48,51,52,55]
N = 4
import mx_ref
BF = ml_dtypes.bfloat16
def gentries(a):
    return np.ascontiguousarray(a.reshape(8, 16, -1).transpose(0, 2, 1)).reshape(8, -1)
def gtable(e):
    e = np.asarray(e); return np.ascontiguousarray(e.reshape(8, -1, 16).transpose(0, 2, 1)).reshape(128, -1).astype(np.int32)
def gcols(t, e):
    v = np.concatenate([t.reshape(8, 16, -1, 4), np.zeros((8, 16, 1, 4), BF)], axis=2)
    return np.ascontiguousarray(np.stack([v[g][:, e[g]] for g in range(8)])).reshape(128, -1)
def tile(rs):
    return np.stack(rs, axis=2).reshape(128, -1).astype(BF)
def pick(q, e):
    c = np.concatenate([q[0].reshape(128, -1, 4), np.zeros((128, 1, 4), np.uint8)], axis=1); s = np.concatenate([q[1], np.ones((16, 1), np.uint8)], axis=1)
    return (np.ascontiguousarray(c[:, e].reshape(128, -1)), np.ascontiguousarray(s[:, e]))
def join(*qs):
    return (np.concatenate([q[0] for q in qs], axis=1), np.concatenate([q[1] for q in qs], axis=1))
def put(q, e, v):
    c, s = q[0].reshape(128, -1, 4).copy(), q[1].copy(); c[:, e] = v[0].reshape(128, -1, 4); s[:, e] = v[1]
    return (c.reshape(128, -1), s)
def pk(c, s):
    return (np.ascontiguousarray(c), mx_ref.live(s))
def emit(q):
    return q[0], q[1]
def packed(v, rng):
    q = [mx_ref.quantize(np.ascontiguousarray(v[r])) for r in range(N)]
    return np.stack([a for a, b in q]), np.stack([mx_ref.plane(b, rng) for a, b in q])
def values_of_codes():
    e, c = np.zeros((128, 128, 4), np.float32), np.zeros((128, 2, 4), np.uint8)
    e[np.arange(128), np.arange(128), 0] = 1
    c[:127, :, 0] = np.arange(256).reshape(2, 128).T[:127]
    return mx_ref.matmul(mx_ref.quantize(e.reshape(128, 512).astype(BF)), (c.reshape(128, 8), np.full((16, 2), 127, np.uint8))).T.reshape(-1).astype(np.float64)
CODE_VALUE, SCALE_VALUE = values_of_codes(), 2.0 ** (np.arange(256) - 127.0)
def decode(q):
    return (CODE_VALUE[q[0]].reshape(16, 8, -1, 4) * SCALE_VALUE[q[1]][:, None, :, None] + 0.0).reshape(128, -1).astype(np.float32)
def f(rng, *shape):
    return mx_ref.flush((rng.standard_normal(shape, dtype=np.float32) * np.exp2(rng.integers(-2, 3, shape[:-1] + (1,)))).astype(BF))
def wide(rng, *shape, cols=0):
    v = rng.standard_normal(shape, dtype=np.float32) * np.exp2(rng.integers(-12, 13, shape)).astype(np.float32)
    if cols: v *= np.repeat(np.exp2(rng.integers(-cols, cols + 1, shape[:-2] + (1, shape[-1] // 4))) * (rng.random(shape[:-2] + (1, shape[-1] // 4)) > 0.0625), 4, axis=-1).astype(np.float32)
    return mx_ref.flush(v.astype(BF))
C, GW, R, SWEEPS = 384, 96, 3, 6
JUMP = [0, 1, 4]
def big(v):
    v = v.astype(np.float32)
    v[np.abs(v) < np.float32(2.0 ** -16)] = 0
    return v.astype(BF)
def numbers_of(rng):
    return {"x": big(f(rng, N, 128, 4 * C)), "u": np.array(f(rng, N, 128, 512)), "v": np.array(f(rng, N, 128, 512))}
def weights(rng, still=[]):
    w = big(f(rng, N, 128, 2048)).reshape(N, 8, 16, 4, 8, 16, 4)
    for i in still:
        w[:, :, i] = 0
        w[:, :, :, :, :, i] = 0
    c, p = packed(w.reshape(N, 128, 2048), rng)
    return {"wc": c, "ws": p}
def ltable(a):
    return gtable(a.transpose(1, 0, 2).reshape(8, 3 * C))
def drawn(rng):
    a = np.zeros((3, 8, C), np.int64)
    for g in range(8):
        o = rng.permutation(C)
        a[0, g, o[::2]] = o[1::2]
        a[0, g, o[1::2]] = o[::2]
        for k in (1, 2):
            if g & JUMP[k] == 0:
                o = rng.permutation(C)
                a[k, g] = o
                a[k, g ^ JUMP[k], o] = np.arange(C)
    return a
def links(rng):
    return np.stack([ltable(drawn(rng)) for r in range(N)])
def setup_inputs(rng):
    return {**numbers_of(rng), "lk": links(rng), **weights(rng)}
def setup_inputs_ties(rng):
    d = numbers_of(rng)
    x = d["x"].reshape(N, 8, 16, C, 4)
    x[:, :, 0] = 0
    x[:, :, 0, :, 0] = rng.integers(0, 4, (N, 8, C)).astype(np.float32).astype(BF)
    u = d["u"].reshape(N, 128, 128, 4)
    u[:, :, ::16] = 0
    o = rng.permutation(N)
    for r in range(N):
        for h in range(0, 128, 16): u[r, h, h, 0] = 0.0 if r == o[0] else -1.0 if r == o[1] else 1.0
    return {"x": x.reshape(N, 128, 4 * C), "u": u.reshape(N, 128, 512), "v": d["v"], "lk": links(rng), **weights(rng, [0])}
def setup_inputs_near(rng):
    d = numbers_of(rng)
    x = d["x"].astype(np.float32).reshape(N, 8, 16, C, 4)
    x[:, :, 0] = 0
    x[:, :, 8:] = 0
    x[:, :, 0, :, 0] = 1
    s = rng.integers(0, 16, (N, 8, C))
    x[:, :, 8] = ((s[:, :, :, None] >> np.arange(4)) & 1) * np.exp2(np.arange(4) - 21.0)
    x[:, :, 11, :, 0] = 2.0 ** -10
    u = d["u"].reshape(N, 128, 128, 4)
    u[:, :, ::16] = 0
    o = rng.permutation(N) % 4
    for r in range(N):
        far = rng.permutation(8)
        if o[r] == 0: x[r, :, 0, :, 0] = 7
        if o[r] == 1: x[r, :, 0, :, 0] = -1
        if o[r] < 2:
            for i in range(4): x[r, far[i], 0, rng.integers(C), 0] = (-1.5 if i == 0 else 1.5) * 2.0 ** 29
        if o[r] == 3:
            x[r, :, 8:] = 0
            x[r, :, 10, :, 0] = (8 + rng.integers(0, 8, (8, C))) * 2.0 ** -33
        k = 1.0 if o[r] == 0 else 2.0 ** -30
        for g in range(8):
            h = 16 * g
            if o[r] < 2:
                u[r, h, h, 0] = k
                u[r, h + 11, h, 0] = k
            if o[r] == 2 and g == far[0]: u[r, h, h, 0] = 1.0
            if o[r] == 2 and g == far[1]: u[r, h, h, 0] = -1.0
            if o[r] < 3: u[r, h + 8, h] = k
            else: u[r, h + 10, h, 0] = k * 1.125 if g >= 4 else k
    return {"x": x.reshape(N, 128, 4 * C).astype(BF), "u": u.reshape(N, 128, 512), "v": d["v"], "lk": links(rng), **weights(rng, [0, 8, 9, 10, 11, 12, 13, 14, 15])}
def setup_inputs_cubes(rng):
    d = numbers_of(rng)
    x = d["x"].reshape(N, 8, 16, C, 4)
    x[:, :, 0] = 0
    low = (1.125 + 0.25 * rng.integers(0, 4, (N, 8, 8, C, 4))) * np.exp2(10.0 - rng.integers(8, 15, (N, 8, 8, C, 4)))
    x[:, :, 8:] = (low * rng.choice([-1.0, 1.0], (N, 8, 8, C, 4))).astype(np.float32).astype(BF)
    x[:, :, 8, :, 0] = 2016.0
    u = d["u"].reshape(N, 128, 128, 4)
    u[:, :, ::16] = 0
    p, e = [], rng.permutation(N)
    for r in range(N):
        o = rng.permutation(C) if e[r] % 2 else np.arange(C)
        k = np.zeros(C, np.float32)
        k[o] = np.repeat(rng.integers(-7, 8, C // 2), 2)
        x[r, :, 0, :, 0] = k.astype(BF)
        a = np.tile(np.arange(C), (3, 8, 1))
        a[0][:, o] = o[np.arange(C) ^ 1]
        p.append(ltable(a))
        for h in range(0, 128, 16): u[r, h, h, 0] = -1.0 if e[r] == 0 else 1.0
    w = big(f(rng, N, 128, 2048)).reshape(N, 8, 16, 4, 8, 16, 4)
    w[:, :, 0] = 0
    w[:, :, 8, :, :, :, 0] = 0
    w[:, :, :, :, :, 0] = 0
    w[:, :, :, :, :, 8:] = 0
    for g in range(8): w[:, g, 8, 0, g, 8, 0] = -1.0
    c, s = packed(w.reshape(N, 128, 2048), rng)
    return {"x": x.reshape(N, 128, 4 * C), "u": u.reshape(N, 128, 512), "v": d["v"], "lk": np.stack(p), "wc": c, "ws": s}
def setup_inputs_ends(rng):
    d = numbers_of(rng)
    o = rng.permutation(N) % 4
    a, b = np.flatnonzero(o < 2)[:2]
    o[[a + 1, b]] = o[[b, a + 1]]
    sg = rng.choice([-1.0, 1.0], N)
    x = np.ones((N, 8, 16, C, 4))
    u = d["u"].astype(np.float32).reshape(N, 8, 16, 8, 16, 4)
    u[:, :, :, :, 0] = 0
    v = rng.choice([-1.0, 1.0], (N, 128, 512))
    w = np.zeros((N, 128, 4, 128, 4), np.float32)
    i, p = np.arange(128), []
    for r in range(N):
        large = o[r] < 2
        size = 2.0 ** 30 if large else 2.0 ** -30
        h = rng.permutation(8)
        x[r, h[4:]] = rng.choice([1.0, 0.875, 0.75] if large else [1.0, 1.125, 1.25], (4, 1, C, 1))
        x[r] *= sg[r] * size
        v[r] *= size
        k = size * sg[r] * (1.0 if o[r] % 2 == 0 else -1.0)
        for g in range(8):
            for c in (h[:4] if g in h[:4] else h): u[r, c, :, g, 0] = k
        for b in range(4): w[r, i, b, i, b] = sg[r] * sg[r - 1] * (-2.0 if large else 2.0)
        a = drawn(rng)
        if large:
            a[:2] = C - 1 - np.arange(C)
            a[2] = np.arange(C)
        p.append(ltable(a))
    c, s = packed(w.reshape(N, 128, 2048).astype(BF), rng)
    return {"x": x.reshape(N, 128, 4 * C).astype(np.float32).astype(BF), "u": u.reshape(N, 128, 512).astype(BF), "v": v.astype(np.float32).astype(BF), "lk": np.stack(p), "wc": c, "ws": s}
def setup_inputs_spread(rng):
    d = setup_inputs(rng)
    d["x"] = big(wide(rng, N, 128, 4 * C, cols=6))
    return d
def check_inputs(d):
    b = []
    for k in ("x", "u", "v"):
        a = np.abs(d[k].astype(np.float32))
        if not (np.isfinite(a).all() and ((a == 0) | (a >= 2.0 ** -30) & (a <= 2.0 ** 30)).all()): b.append("a value of " + k)
    none, least, most = [emit(mx_ref.quantize(np.full((128, 16), k, np.float32).astype(BF)))[1][0, 0] for k in (0.0, 2.0 ** -16, 2.0 ** 5)]
    for r in range(N):
        e = gentries(d["lk"][r])
        if not ((e >= 0) & (e < C)).all(): b.append("an entry of lk")
        else:
            n = other_ends(d["lk"][r])
            if (np.take_along_axis(n, n, axis=1) != np.arange(8 * C)).any(): b.append("a link of lk isn't the same from both ends")
            if (n == np.arange(8 * C)).any(): b.append("a link of lk from a node to itself")
        if ((d["wc"][r] == 0x7F) | (d["wc"][r] == 0xFF)).any(): b.append("wc: a code that is no number")
        s = mx_ref.live(d["ws"][r])
        if ((s != none) & ((s < least) | (s > most))).any(): b.append("ws: a scale out of range")
    return b
def other_ends(a):
    e = gentries(a).reshape(8, 3, C).astype(np.int64)
    return np.stack([(e[:, k] + C * (np.arange(8) ^ JUMP[k])[:, None]).reshape(-1) for k in range(3)])
def parts(t):
    return t.reshape(8, 16, -1, 4).transpose(0, 2, 1, 3).reshape(-1, 16, 4)
def whole(p):
    return np.ascontiguousarray(p.reshape(8, -1, 16, 4).transpose(0, 2, 1, 3)).reshape(128, -1)
def reference(x, u, v, lk, wc, ws):
    qu = [mx_ref.quantize(u[r]) for r in range(N)]
    lay = [pk(wc[r], ws[r]) for r in range(N)]
    ends = [other_ends(lk[r]) for r in range(N)]
    now = [x[r] for r in range(N)]
    node = np.arange(8 * C)
    away, mark = [None] * N, [np.zeros((3, 8 * C), bool) for r in range(N)]
    route = [None] * N
    for t in range(R):
        sent, blend, gate = [], [], []
        for r in range(N):
            q, n = mx_ref.quantize(now[r]), ends[r]
            s = mx_ref.matmul(qu[r], q)[::16] + np.float32(0.0)
            l = np.argsort(s, axis=1, kind="stable")[:, :GW]
            slot = np.full((8, C), -1)
            np.put_along_axis(slot, l, np.tile(np.arange(GW), (8, 1)), axis=1)
            slot, s = slot.reshape(-1), s.reshape(-1)
            a, m = away[r], mark[r]
            if t == 0: a = (s[n] < s) | (s[n] == s) & (n < node)
            for i in range(SWEEPS):
                sink = ~a.any(axis=0) & (slot < 0)
                turn = sink & (~m | m.all(axis=0))
                came = np.take_along_axis(turn, n, axis=1)
                a = (a | turn) & ~came
                m = (m & ~sink) | came
            away[r], mark[r] = a, m
            k = np.argmin(np.where(a, s[n], np.float32(np.inf)), axis=0)
            to = np.where((slot < 0) & a.any(axis=0), n[k, node], node)
            e = to[to]
            e = e[e]
            own = decode(q)
            p = parts(own)
            blend.append(((p[to] + p[e]) * np.float32(0.5)).astype(BF))
            sent.append(mx_ref.quantize(gcols(own.astype(BF), l)))
            gate.append(slot)
            route[r] = e
        for r in range(N):
            h = parts(tile([mx_ref.matmul(pick(lay[r], np.arange(128 * b, 128 * b + 128)), sent[r - 1]) * np.float32(0.015625) for b in range(4)]))
            z, e, k = blend[r], route[r], gate[r][route[r]]
            w = k >= 0
            z[w] = (z[w].astype(np.float32) + h[GW * (e[w] // C) + k[w]].astype(np.float32)).astype(BF)
            now[r] = whole(z)
    y, nd = np.zeros((N, 128, C), np.float32), np.zeros((N, 8, 2 * C), np.float32)
    oc, osc = np.zeros((N, 128, 4 * C), np.uint8), np.zeros((N, 16, C), np.uint8)
    for r in range(N):
        q = mx_ref.quantize(now[r])
        y[r] = mx_ref.matmul(mx_ref.quantize(v[r]), q)
        nd[r, :, :C] = route[r].reshape(8, C)
        a, m = away[r].astype(np.int64), mark[r].astype(np.int64)
        nd[r, :, C:] = (a[0] + 2 * a[1] + 4 * a[2] + 8 * m[0] + 16 * m[1] + 32 * m[2]).reshape(8, C)
        oc[r], osc[r] = emit(q)
    return {"y": y, "nd": nd, "oc": oc, "osc": osc}

@@ -1,0 +1,713 @@
+import math
+from concourse.bass import DstId, RemoteDMATransfer
+from concourse.mybir import dt, AluOpType, AxisListType, ActivationFunctionType
+
+OP = AluOpType
+COPY = ActivationFunctionType.Copy
+C, GW, R, SWEEPS = 384, 96, 3, 6
+JUMP = [0, 1, 4]
+
+TILES = ["gone", "qsel", "qneg", "q3", "q1_0", "q1_1", "q1_2", "st0", "st1", "st2", "sto", "came0", "came1", "came2",
+         "own0", "own1", "own2", "hop0", "hop1", "hop2", "cls0", "cls1", "cls2", "cls3", "hopf0", "hopf1", "hopf2", "ge", "gm", "gb"]
+TI = {n: i for i, n in enumerate(TILES)}
+NT = len(TILES)
+VSWEEP = [0, 448, 352, 320, 224, 512]
+VHOP = 512
+SLOTS = [3, 3, 3, 3, 3, 3, 4, 6, 0]
+FFIRST = 3
+SSHARE = 0
+ENGINES = 8
+
+F32, BF, I32, U16, X4, U8 = "float32", "bfloat16", "int32", "uint16", "float8_e4m3fn_x4", "uint8"
+SCRATCH = {}
+WIDE = {"KF": "JM MD ND IJF CMr RM J4 J0 J1 J2 D0 D1 D2", "KI": "PC UL WL", "XI": "EI EP",
+        "XF": "SB1 ST SB2 ST2 SB3 ST3 t0 t1 t2 ua ub PE la lb lc qa qb qd qm JF SJF ea eb ec ba bb",
+        "XB": "G3 G9 MA MB MC TU R0 R1 R2 va0 va1 va2 mx0 mx1 mx2 pk0 pk1 pk2 self SJ PP OC0 OC1 OC2 JC EQ LT LE ML"}
+HOME = {n: w for w in WIDE for n in WIDE[w].split()}
+PLACE, LEN = {}, {}
+
+
+def sb(name, n, d):
+    w = HOME.get(name, name)
+    a = SCRATCH[w][1][1] if w in SCRATCH else 0
+    PLACE[name], LEN[name] = (w, a), n
+    SCRATCH[w] = ("sbuf", [128, a + (n if w == name else (n + 15) // 16 * 16)], d)
+
+
+def mx(name, n):
+    sb(name + "c", n, X4)
+    sb(name + "s", n, U8)
+
+
+for _n, _w, _d in [
+        ("X0", 1536, BF), ("X1", 1536, BF), ("U", 512, BF), ("VV", 512, BF),
+        ("LKT", 72, I32), ("LKS", 72, I32), ("OFT", 72, U16), ("OFJ", 72, U16), ("OFS", 72, U16),
+        ("UL", 24, I32), ("ULo", 24, U16), ("WL", 128, I32), ("WLo", 128, U16),
+        ("PC", 16, I32), ("PF", 48, F32), ("WT", 1024, BF), ("CB", 512 * NT, BF), ("FB", 4 * 516, BF),
+        ("GC", 96, BF), ("GCt", 96, BF), ("GOt", 512, BF),
+        ("JM", C, F32), ("MD", C, F32), ("ND", C, F32), ("MX", C, F32), ("NX", C, F32), ("NS", 24, F32), ("TM", 2 * C, BF), ("IJF", C, F32),
+        ("CMr", 96, F32), ("RM", 96, F32), ("J4", 96, F32), ("J0", 96, F32), ("J1", 96, F32), ("J2", 96, F32), ("KM", 32, BF), ("GH", 96, BF), ("qm", C, F32),
+        ("TS", 3 * C, F32), ("SB1", C, F32), ("ST", C, F32), ("EQ", C, BF), ("ET", 4 * C, BF),
+        ("GT", 512, BF), ("G3", 96, BF), ("G9", 96, BF), ("PLo", 24, U16), ("LW", C, F32), ("SB2", C, F32),
+        ("ST2", C, F32), ("SB3", GW, F32), ("ST3", GW, F32), ("ELo", 6, U16),
+        ("FT", 16 * C, BF), ("HT", 16 * C, BF), ("SL", 4 * C, F32), ("FD", 4 * C, BF), ("Z", 4 * C, BF),
+        ("LT", C, BF), ("LE", C, BF), ("ML", C, BF), ("AW", 1280, BF), ("RF", 1280, BF), ("NB", 2 * C, F32),
+        ("MA", 96, BF), ("MB", 96, BF), ("MC", 96, BF), ("IN", 512, BF), ("TU", 96, BF), ("W", 512, BF), ("GA", 1280, BF),
+        ("R0", 96, BF), ("R1", 96, BF), ("R2", 96, BF), ("va0", 96, BF), ("va1", 96, BF), ("va2", 96, BF),
+        ("mx0", 96, BF), ("mx1", 96, BF), ("mx2", 96, BF), ("pk0", 96, BF), ("pk1", 96, BF), ("pk2", 96, BF),
+        ("self", 96, BF), ("SJ", 96, BF), ("SJF", 96, F32), ("t0", 96, F32), ("t1", 96, F32), ("t2", 96, F32),
+        ("ua", 96, F32), ("ub", 96, F32), ("PP", 96, BF), ("PE", 96, F32),
+        ("la", 96, F32), ("lb", 48, F32), ("lc", 24, F32), ("DL", 24, U16), ("EL", 24, U16), ("HL", 24, U16),
+        ("D0", C, F32), ("D1", C, F32), ("D2", C, F32), ("CTF", C, F32),
+        ("qa", C, F32), ("qb", 192, F32), ("qd", 96, F32), ("OC0", 96, BF), ("OC1", 96, BF), ("OC2", 96, BF), ("JC", 96, BF), ("JF", 96, F32),
+        ("ea", 96, F32), ("eb", 96, F32), ("ec", 96, F32), ("EI", 96, I32), ("EP", 288, I32), ("ba", 96, F32), ("bb", 96, F32),
+        ]:
+    sb(_n, _w, _d)
+for _n, _w in [("QX", C), ("QU", 128), ("QUP", C), ("QV", 128), ("WC", 512), ("WP", 2048), ("QK", 128 * NT), ("QF", 2048),
+               ("QT", 7 * C), ("QG", 128), ("QAW", 320), ("QRF", 320), ("QIN", 128), ("QGA", 320), ("QW", 128),
+               ("QE", 3 * 128), ("LD", 320), ("QND", C)]:
+    mx(_n, _w)
+for _i in range(7):
+    if _i < 4:
+        sb("C%d" % _i, 4 * C, BF)
+for _i in range(R):
+    sb("E%d" % _i, 512, BF)
+PS = ["PV0", "PV1", "PV2", "PV3", "PA", "PB", "PCC", "PD"]
+for _n in PS:
+    SCRATCH[_n] = ("psum", [128, 512], F32)
+    PLACE[_n], LEN[_n] = (_n, 0), 512
+SEMAPHORES = ["sv", "ss", "st", "sg", "lcl", "arr0", "arr1", "arr2"] + ["d%d" % i for i in range(16)]
+
+
+def rank_program(g, core, T, topo):
+    rank = T.rank_of(core)
+    if rank is None:
+        return
+    nxt = T.cores[(rank + 1) % len(T.cores)]
+    Q = {"V": g.vector, "S": g.scalar, "T": g.tensor, "G": g, "Y": g.sync}
+    SEM = {"V": "sv", "S": "ss", "T": "st", "G": "sg"}
+    cnt = {s: 0 for s in SEMAPHORES}
+    known = {q: {} for q in Q}
+    clk, wrs, rds, bank = {}, {}, {}, {}
+
+    def overlap(a, b):
+        if a[1] <= b[0] or b[1] <= a[0]: return False
+        d = math.gcd(a[2], b[2])
+        return not (d > 1 and (a[0] - b[0]) % d)
+
+    def await_(q, deps):
+        best = {}
+        for s, c in deps:
+            best[s] = max(best.get(s, 0), c)
+        for s, c in sorted(best.items(), key=lambda t: -t[1]):
+            if known[q].get(s, 0) >= c: continue
+            Q[q].wait_ge(T.sem[s], c)
+            known[q][s] = c
+            for s2, c2 in clk[(s, c)].items():
+                if known[q].get(s2, 0) < c2: known[q][s2] = c2
+
+    def deps_of(q, rd, wr):
+        deps = []
+        for n, lo, hi, st in rd:
+            if n in PS: continue
+            for e in wrs.get(n, []):
+                if overlap(e[0], (lo, hi, st)): deps.append(e[1])
+        for n, lo, hi, st in wr:
+            if n in PS: continue
+            for e in wrs.get(n, []):
+                if overlap(e[0], (lo, hi, st)): deps.append(e[1])
+            for e in rds.get(n, []):
+                if overlap(e[0], (lo, hi, st)): deps.append(e[1])
+        for n in set(x[0] for x in list(rd) + list(wr) if x[0] in PS):
+            for q2, m in bank.get(n, {}).items():
+                if q2 != q: deps.append(m)
+        return deps
+
+    def record(q, m, rd, wr):
+        for n, lo, hi, st in wr:
+            if n in PS: continue
+            for tab in (wrs, rds):
+                tab[n] = [e for e in tab.get(n, []) if not (e[0][0] >= lo and e[0][1] <= hi and (st == 1 or (e[0][2] == st and e[0][0] == lo)))]
+            wrs[n].append(((lo, hi, st), m, q))
+        for n, lo, hi, st in rd:
+            if n in PS: continue
+            rds[n] = [e for e in rds.get(n, []) if not (e[2] == q and q != "D" and e[0] == (lo, hi, st))] + [((lo, hi, st), m, q)]
+        for n in set(x[0] for x in list(rd) + list(wr) if x[0] in PS):
+            b = bank.get(n, {})
+            b = {q2: m2 for q2, m2 in b.items() if q2 == q or known[q].get(m2[0], 0) < m2[1]}
+            b[q] = m
+            bank[n] = b
+
+    def do(q, fn, rd, wr):
+        await_(q, deps_of(q, rd, wr))
+        s = SEM[q]
+        cnt[s] += 1
+        m = (s, cnt[s])
+        fn(Q[q]).then_inc(T.sem[s], 1)
+        c = dict(known[q])
+        c[s] = cnt[s]
+        clk[m] = c
+        record(q, m, rd, wr)
+
+    def dma(q, s, pairs, rd=(), wr=()):
+        await_(q, deps_of("D", rd, wr))
+        for o, i in pairs:
+            Q[q].dma_start(o, i).then_inc(T.sem[s], 16)
+            cnt[s] += 16
+        m = (s, cnt[s])
+        c = dict(known[q])
+        c[s] = cnt[s]
+        clk[m] = c
+        record("D", m, rd, wr)
+
+    def r(n, lo=0, hi=None, st=1):
+        w, a = PLACE[n]
+        return (w, a + lo, a + (LEN[n] if hi is None else hi), st)
+
+    def ap(x):
+        n, lo, hi, st = x
+        return T[n][:, lo:hi] if st == 1 else T[n][:, lo:hi:st]
+
+    isr = lambda x: isinstance(x, tuple)
+    val = lambda x: ap(x) if isr(x) else x
+
+    def ts(o, i, s1, op0, s2=None, op1=None):
+        rd = [i] + [s for s in (s1, s2) if isr(s)]
+        if op1 is None: do("V", lambda e: e.tensor_scalar(ap(o), ap(i), val(s1), None, op0), rd, [o])
+        else: do("V", lambda e: e.tensor_scalar(ap(o), ap(i), val(s1), val(s2), op0, op1), rd, [o])
+
+    def tt(o, a, b, op, off=None):
+        if off is None: do("V", lambda e: e.tensor_tensor(ap(o), ap(a), ap(b), op), [a, b], [o])
+        else: do("V", lambda e: e.tensor_tensor(ap(o), ap(a).indirect(ap(off)), ap(b), op), [a, b, off], [o])
+
+    def tc(o, a, off=None):
+        if off is None: do("V", lambda e: e.tensor_copy(ap(o), ap(a)), [a], [o])
+        else: do("V", lambda e: e.tensor_copy(ap(o), ap(a).indirect(ap(off))), [a, off], [o])
+
+    def act(o, a, bias=0.0, scale=1.0, off=None):
+        rd = [a] + [x for x in (scale, off) if isr(x)]
+        if off is None: do("S", lambda e: e.activation(ap(o), ap(a), COPY, bias=bias, scale=val(scale)), rd, [o])
+        else: do("S", lambda e: e.activation(ap(o), ap(a).indirect(ap(off)), COPY, bias=bias, scale=val(scale)), rd, [o])
+
+    def scan(o, a, b):
+        do("V", lambda e: e.tensor_tensor_scan(ap(o), ap(a), ap(b), 0.0, OP.mult, OP.add), [a, b], [o])
+
+    def fill(o, c):
+        do("V", lambda e: e.memset(ap(o), c), [], [o])
+
+    def quant(n, a, b, src):
+        q, s = r(n + "c", a, b), r(n + "s", a, b)
+        do("V", lambda e: e.quantize_mx(ap(q), ap(s), ap(src)), [src], [q, s])
+
+    def mm(bk, st, mv, n, start=True, stop=True):
+        l, ls = r(st[0] + "c", st[1], st[1] + 128), r(st[0] + "s", st[1], st[1] + 128)
+        m, ms = r(mv[0] + "c", mv[1], mv[1] + n), r(mv[0] + "s", mv[1], mv[1] + n)
+        o = r(bk, 0, n)
+        do("T", lambda e: e.matmul_mx(ap(o), ap(l), ap(ls), ap(m), ap(ms), start, stop), [l, ls, m, ms], [o])
+
+    def iota(o, pat, base, cm):
+        fl = SCRATCH[o[0]][2] != I32
+        if fl: do("G", lambda e: e.iota(ap(o), pat, base, cm, allow_small_or_imprecise_dtypes=True), [], [o])
+        else: do("G", lambda e: e.iota(ap(o), pat, base, cm), [], [o])
+
+    def sel(o, i, pat, op, fl, base, cm):
+        do("G", lambda e: e.affine_select(ap(o), ap(i), pat, op, fl, base, cm), [i], [o])
+
+    K = lambda n: ("QK", 128 * TI[n])
+    tile0 = lambda n: 512 * TI[n]
+
+    dma("Y", "d0", [(T.X0[:], T.x[:])], wr=[r("X0")])
+    dma("S", "d1", [(T.U[:], T.u[:])], wr=[r("U")])
+    dma("Y", "d2", [(T.LKT[:], T.lk[:])], wr=[r("LKT")])
+    pr = [(T.LKS[:, 0:24], T.lk[:, 0:24])]
+    for h in range(8):
+        a = h ^ JUMP[1]
+        pr.append((T.LKS[16 * h:16 * h + 16, 24:48], T.lk[16 * a:16 * a + 16, 24:48]))
+    for h in range(0, 8, 4):
+        a = h ^ JUMP[2]
+        pr.append((T.LKS[16 * h:16 * h + 64, 48:72], T.lk[16 * a:16 * a + 64, 48:72]))
+    dma("Y", "d3", pr, wr=[r("LKS")])
+    dma("Y", "d4", [(T.WCc[:].bitcast(dt.uint8), T.wc[:]), (T.WCs[:], T.ws[:])], wr=[r("WCc"), r("WCs")])
+    dma("Y", "d5", [(T.VV[:], T.v[:])], wr=[r("VV")])
+
+    GRP = {0: ([[16, 8]], 0), 1: ([[32, 4], [-16, 2]], 16), 4: ([[-64, 2], [16, 4]], 64)}
+    neg = lambda pat: [[-a, b] for a, b in pat]
+    for k in range(3):
+        iota(r("UL", 8 * k, 8 * k + 8), GRP[JUMP[k]][0], GRP[JUMP[k]][1], 0)
+    iota(r("PC", 0, 1), [[0, 1]], 0, 1)
+    iota(r("JM"), [[0, 24], [1, 16]], 0, 0)
+    fill(r("WT", 0, 512), 1.0)
+    for j, w in enumerate([-6.0, -2.0, 3.0, -1.0]):
+        fill(r("WT", 512 + 128 * j, 640 + 128 * j), w)
+    WCOL = {1.0: 0, -6.0: 512, -2.0: 640, 3.0: 768, -1.0: 896}
+    tc(r("ULo"), r("UL"))
+    fill(r("FB"), 0.0)
+    PFC = {}
+
+    def pcol(name):
+        PFC[name] = len(PFC)
+        return r("PF", PFC[name], PFC[name] + 1)
+
+    P = lambda name: r("PF", PFC[name], PFC[name] + 1)
+    p = r("PC", 0, 1)
+    for j, (n, sh, an) in enumerate([("i", 0, 15), ("s", 0, 3), ("kk", 2, 3), ("g0", 4, 1), ("g1", 5, 1), ("g2", 6, 1)]):
+        o = r("PC", j + 1, j + 2)
+        ts(o, p, sh, OP.arith_shift_right, an, OP.bitwise_and)
+        tc(pcol(n), o)
+    ts(r("MD"), r("JM"), P("i"), OP.is_equal)
+    ts(r("ND"), r("JM"), P("i"), OP.not_equal)
+    ts(r("MX"), r("MD"), 2e29, OP.mult, -1e29, OP.add)
+    act(r("NX"), r("MD"), scale=-2e29)
+    for A in range(4):
+        for h in range(2):
+            a = 516 * A + 3 + 256 * h
+            sel(r("FB", a, a + 253, 4), r("WT", 0, 64), [[-32, 2], [0, 2], [-1, 16]], OP.is_equal, 0.0, -(16 * (A & 1) + 64 * (A >> 1)), 1)
+    sel(r("NX"), r("NX"), [[0, 24], [1, 16]], OP.not_equal, -2e29, 0, 0)
+    t0 = tile0("gone")
+    sel(r("GOt"), r("WT", 0, 512), [[-16, 8], [0, 64]], OP.is_ge, 0.0, 0, 1)
+    sel(r("CB", t0, t0 + 512), r("GOt"), [[16, 8], [0, 64]], OP.is_ge, 0.0, 15, -1)
+    quant("QU", 0, 128, r("U"))
+    off = r("ULo")
+    do("V", lambda e: e.tensor_copy(T.QUPc[:, 0:384].bitcast(dt.uint32), T.QUc[:, 0:128].bitcast(dt.uint32).indirect(ap(off))), [r("QUc"), off], [r("QUPc")])
+    def zeros(a, b):
+        while a < b:
+            n = min(1024, b - a)
+            act(r("CB", a, a + n), r("WT", 0, n), scale=0.0)
+            a += n
+
+    zc = tile0("came0")
+    zeros(zc, zc + 2048)
+    do("S", lambda e: e.activation(T.QUPs[:, 0:384], T.QUs[:, 0:128].indirect(ap(off)), COPY), [r("QUs"), off], [r("QUPs")])
+    z0 = tile0("qsel")
+    quant("QX", 0, C, r("X0"))
+
+    def scores():
+        mm("PA", ("QUP", 0), ("QX", 0), C)
+        mm("PB", ("QUP", 0), ("QX", 0), C)
+        mm("PCC", ("QUP", 128), ("QX", 0), C)
+        mm("PD", ("QUP", 256), ("QX", 0), C)
+        act(r("TS", 0, C), r("PB", 0, C))
+        act(r("TS", C, 2 * C), r("PCC", 0, C))
+        act(r("TS", 2 * C, 3 * C), r("PD", 0, C))
+
+    scores()
+    act(r("NB", 0, C), r("PB", 0, C))
+
+    def setup_first():
+        quant("QK", 0, 128, r("CB", 0, 512))
+        for A in range(4):
+            for b in range(4):
+                quant("QF", 512 * A + 128 * b, 512 * A + 128 * b + 128, r("FB", 516 * A + 3 - b, 516 * A + 515 - b))
+
+    zeros(z0, zc)
+    zeros(zc + 2048, tile0("cls0"))
+    for a in (0, 768): act(r("ET", a, a + 768), r("WT", 0, 768), scale=0.0)
+    for n, a in (("GT", C), ("W", C), ("GA", 1152), ("AW", 1152), ("RF", 1152)):
+        fill(r(n, a), 0.0)
+    for t in range(R):
+        fill(r("E%d" % t, 4 * GW, 512), 0.0)
+    fill(r("IN"), 0.0)
+    fill(r("GA", 640, 1152), 0.0)
+    quant("QGA", 192, 320, r("GA", 768, 1280))
+    iota(r("IJF"), [[1, C]], 0, 0)
+
+    def stile(n, c, pat, base, w):
+        gp, gb = GRP[c]
+        for s in range(4):
+            a = tile0(n) + 5 * s
+            o = r("CB", a, tile0(n) + 512, 16)
+            sel(o, r("WT", WCOL[w], WCOL[w] + 32), neg(gp) + pat, OP.is_equal, 0.0, -gb - base - s, 1)
+
+    def otile(n, c, k, w):
+        gp, gb = GRP[c]
+        for s in range(4):
+            o = r("CB", tile0(n) + 16 * k + 5 * s, tile0(n) + 512, 64)
+            sel(o, r("WT", WCOL[w], WCOL[w] + 8), neg(gp), OP.is_equal, 0.0, -gb - 4 * k - s, 1)
+
+    stile("qsel", 0, [[-4, 4]], 0, 1.0)
+    stile("qneg", 0, [[-4, 4]], 0, -1.0)
+    stile("q3", 0, [[-4, 4]], 0, 3.0)
+    for k in range(3): otile("q1_%d" % k, 0, k, 1.0)
+    for k in range(3):
+        for e in (0, 1 + k): sel(r("CB", tile0("st%d" % k) + e, tile0("st%d" % k) + 512, 4), r("WT", WCOL[3.0], WCOL[3.0] + 128), [[-1, 128]], OP.is_equal, 0.0, 0, 1)
+    sel(r("CB", tile0("sto"), tile0("sto") + 512, 4), r("WT", 0, 128), [[-1, 128]], OP.is_equal, 0.0, 0, 1)
+    for k in range(3):
+        for s in range(4): sel(r("CB", tile0("sto") + 16 * k + 4 * s + 1 + k, tile0("sto") + 512, 64), r("WT", 0, 8), [[-16, 8]], OP.is_equal, 0.0, -4 * k - s, 1)
+    for k in range(3):
+        gp, gb = GRP[JUMP[k]]
+        sel(r("GCt", 32 * k, 32 * k + 32), r("WT", 0, 32), neg(gp) + [[0, 4]], OP.is_ge, 0.0, -gb, 1)
+        sel(r("GC", 32 * k, 32 * k + 32), r("GCt", 32 * k, 32 * k + 32), gp + [[0, 4]], OP.is_ge, 0.0, gb + 15, -1)
+    iota(r("CMr"), [[0, 24], [1, 4]], 0, 0)
+    iota(r("D0"), [[0, 48], [1, 8]], 0, 0)
+    iota(r("D1"), [[0, 6], [8, 8], [0, 8]], 0, 0)
+    iota(r("D2"), [[64, 6], [0, 64]], 0, 0)
+    iota(r("J4"), [[4, 96]], 0, 0)
+    iota(r("J0"), [[0, 48], [4, 2]], 0, 0)
+    iota(r("J1"), [[0, 6], [8, 8], [0, 2]], 0, 0)
+    iota(r("J2"), [[64, 6], [0, 16]], 0, 0)
+    iota(r("CB", tile0("hopf0"), tile0("gb") + 512), [[0, 512 * (TI["gb"] + 1 - TI["hopf0"])]], 0, 0)
+    for b in range(4):
+        for A in range(4):
+            a = 32 * b + 8 * A
+            iota(r("WL", a, a + 8), [[0, 2], [32, 2], [0, 2]], 128 * b + 16 * (A & 1) + 64 * (A >> 1), 0)
+    iota(r("HT"), [[0, 16 * C]], 0, 0)
+
+    def quant_tiles(a, b):
+        a, b = TI[a], TI[b] + 1
+        while a < b:
+            n = min(4, b - a)
+            quant("QK", 128 * a, 128 * (a + n), r("CB", 512 * a, 512 * (a + n)))
+            a += n
+
+    def setup_lists():
+        tc(r("OFT", 0, 24), r("LKT", 0, 24))
+        for k in (1, 2): ts(r("OFT", 24 * k, 24 * k + 24), r("LKT", 24 * k, 24 * k + 24), float(C * k), OP.add)
+        tc(r("OFJ"), r("LKT"))
+        tc(r("OFS"), r("LKS"))
+        for s in range(4): ts(pcol("ms%d" % s), P("s"), float(s), OP.is_equal)
+        for k in range(4): ts(pcol("mr%d" % k), P("kk"), float(k), OP.is_equal)
+        for k in range(3):
+            ts(pcol("mc%d" % k), P("mr%d" % k), -6.0, OP.mult)
+            ts(pcol("mw%d" % k), P("mr%d" % k), -2.0, OP.mult)
+        ts(pcol("A"), P("g2"), 2.0, OP.mult)
+        tt(pcol("A2"), P("A"), P("g0"), OP.add)
+        ts(pcol("A384"), P("A2"), 384.0, OP.mult)
+
+    def setup_moves():
+        for k in range(3):
+            for s in range(4):
+                a = tile0("came%d" % k)
+                act(r("CB", a + 5 * s, a + 512, 16), r("GC", 32 * k, 32 * k + 32), scale=P("mc%d" % k))
+                a = tile0("own%d" % k)
+                act(r("CB", a + 16 * k + 5 * s, a + 512, 64), r("GC", 32 * k + k, 32 * k + 32, 4), scale=P("mw%d" % k))
+
+    def setup_classes():
+        for A in range(4):
+            for h in range(4):
+                o, src = tile0("cls%d" % A) + 128 * h, tile0("gone") + 64 * ((A & 1) + 2 * (h & 1) + 4 * (A >> 1))
+                for g0 in range(2): act(r("CB", o + 64 * g0, o + 64 * g0 + 64), r("CB", src, src + 64))
+
+    def setup_hops():
+        ts(r("KM"), r("CMr", 0, 32), P("kk"), OP.is_equal)
+        for k in range(3):
+            tt(r("GH", 32 * k, 32 * k + 32), r("GC", 32 * k, 32 * k + 32), r("KM"), OP.mult)
+            for s in range(4):
+                a = tile0("hop%d" % k) + 5 * s
+                act(r("CB", a, tile0("hop%d" % k) + 512, 16), r("GH", 32 * k, 32 * k + 32))
+                a = tile0("hopf%d" % k) + 5 * s
+                act(r("CB", a, tile0("hopf%d" % k) + 512, 16), r("GC", 32 * k, 32 * k + 32))
+        for e, n in ((0, "ge"), (1, "ge"), (2, "gm"), (3, "gb")):
+            act(r("CB", tile0(n) + e, tile0(n) + 512, 4), r("CB", tile0("gone") + e, tile0("gone") + 512, 4))
+
+    def setup_routes():
+        ts(r("RM"), r("CMr"), P("kk"), OP.is_equal)
+        for d in range(3): act(r("D%d" % d), r("D%d" % d), scale=P("mr%d" % d))
+        tt(r("qa"), r("D0"), r("D1"), OP.add)
+        tt(r("CTF"), r("qa"), r("D2"), OP.add)
+        tt(pcol("a3s"), P("A384"), P("mr3"), OP.mult)
+        for k, n, f in ((1, "g0", 384.0), (2, "g2", 768.0)):
+            ts(pcol("x%d" % k), P(n), -2.0 * f, OP.mult, f, OP.add)
+            tt(pcol("y%d" % k), P("x%d" % k), P("A384"), OP.add)
+            tt(pcol("z%d" % k), P("y%d" % k), P("mr3"), OP.mult)
+
+        ts(r("JF"), r("J4"), P("s"), OP.add, P("A384"), OP.add)
+        ts(r("t0"), r("J0"), P("s"), OP.add, P("mr0"), OP.mult)
+        ts(r("t1"), r("J1"), P("mr1"), OP.mult, P("a3s"), OP.add)
+        ts(r("t2"), r("J2"), P("mr2"), OP.mult)
+        tt(r("ua"), r("t0"), r("t1"), OP.add)
+        tt(r("JC"), r("ua"), r("t2"), OP.add)
+
+    def setup_ends(k):
+        act(r("qa"), r("CTF"), off=r("OFJ", 24 * k, 24 * k + 24))
+        for s in range(4): act(r("qm", 96 * s, 96 * s + 96), r("qa", s, C, 4), scale=P("ms%d" % s))
+        tt(r("qb"), r("qm", 0, 192), r("qm", 192, C), OP.add)
+        tt(r("qd"), r("qb", 0, 96), r("qb", 96, 192), OP.add)
+        ts(r("OC%d" % k), r("qd"), P("a3s") if k == 0 else P("z%d" % k), OP.add)
+
+    def setup_layer():
+        ts(r("WLo"), r("WL"), P("i"), OP.add)
+        wo = r("WLo")
+        do("V", lambda e: e.tensor_copy(T.WPc[:, 0:2048].bitcast(dt.uint32), T.WCc[:, 0:512].bitcast(dt.uint32).indirect(ap(wo))), [r("WCc"), wo], [r("WPc")])
+        do("S", lambda e: e.activation(T.WPs[:, 0:2048], T.WCs[:, 0:512].indirect(ap(wo)), COPY), [r("WCs"), wo], [r("WPs")])
+
+    setup_lists()
+    ts(pcol("h768"), P("g1"), 768.0, OP.mult)
+    ts(pcol("two"), P("mr1"), 2.0, OP.mult)
+    ts(pcol("four"), P("mr2"), 4.0, OP.mult)
+    tt(pcol("six"), P("two"), P("four"), OP.add)
+    tt(pcol("bit"), P("six"), P("mr0"), OP.add)
+    ts(pcol("bit8"), P("bit"), 8.0, OP.mult)
+    for s in range(4): tt(pcol("mo%d" % s), P("ms%d" % s), P("mr0"), OP.mult)
+
+    def masked(src, wdt="W"):
+        for s in range(4):
+            o = r("W", s, C, 4)
+            if s < 2: ts(o, src, P("ms%d" % s), OP.mult)
+            else: act(o, src, scale=P("ms%d" % s))
+
+    def gather_w(n):
+        v = n // 16
+        win = r("W", 0, C)
+        act(r("GA", n, 1152), win, off=r("OFS", v, 72))
+        if n: tc(r("GA", 0, n), win, off=r("OFS", 0, v))
+
+    def to_list(src, o):
+        tt(r("la"), src, r("RM"), OP.mult)
+        tt(r("lb"), r("la", 0, 96, 2), r("la", 1, 96, 2), OP.add)
+        tt(r("lc"), r("lb", 0, 48, 2), r("lb", 1, 48, 2), OP.add)
+        tc(o, r("lc"))
+
+    def send(t):
+        m = topo.engines(core, nxt)[:ENGINES]
+        mask = sum(1 << e for e in m)
+        rid, pid, _ = topo.addr(nxt)
+        n = 128 if t == 0 else GW
+        a = 0 if t == 0 else 32 + GW * t
+        c, s = r("QEc", 128 * t, 128 * t + n), r("QEs", 128 * t, 128 * t + n)
+        await_("G", deps_of("D", [c, s], []))
+        sem = T.sem["arr%d" % t]
+        g.remote_dma(T.LDc[:, a:a + n].bitcast(dt.uint8), T.QEc[:, 128 * t:128 * t + n].bitcast(dt.uint8), sem, T.sem.lcl, pid, rid, mask)
+        g.remote_dma(T.LDs[:, a:a + n], T.QEs[:, 128 * t:128 * t + n], sem, T.sem.lcl, pid, rid, mask)
+        cnt["lcl"] += 2 * len(m)
+        pe = len(topo.engines(T.cores[(rank - 1) % len(T.cores)], core)[:ENGINES])
+        cnt["arr%d" % t] = 2 * pe
+        clk[("arr%d" % t, 2 * pe)] = {}
+        record("D", ("arr%d" % t, 2 * pe), [], [r("LDc", a, a + n), r("LDs", a, a + n)])
+
+    def state():
+        for k in range(3): act(r("IN", 1 + k, 4 * 96, 4), r("PV%d" % k, 0, 96), scale=1.0 / 3.0)
+
+    def inject(stop):
+        for k in range(3): mm("PV%d" % k, K("st%d" % k), ("QIN", 0), 128, True, stop)
+        mm("PV3", K("sto"), ("QIN", 0), 128, True, stop)
+
+    def number_parts():
+        ts(r("ea"), r("PE"), 768.0, OP.is_ge, 768.0, OP.mult)
+        tt(r("eb"), r("PE"), r("ea"), OP.add)
+        ts(r("ec"), r("eb"), P("h768"), OP.add)
+        tc(r("EI"), r("ec"))
+        for e, m in enumerate((15, 240, 3840)): ts(r("EP", 96 * e, 96 * e + 96), r("EI"), m, OP.bitwise_and)
+        tc(r("qa", 0, 288), r("EP"))
+        tt(r("ea"), r("ba"), r("bb"), OP.add)
+        for s in range(4):
+            for e in range(3): act(r("ET", 4 * s + e, 4 * C, 16), r("qa", 96 * e, 96 * e + 96), scale=P("mo%d" % s))
+            act(r("ET", 4 * s + 3, 4 * C, 16), r("ea"), scale=P("ms%d" % s))
+
+    rot = [0]
+    for t in range(R):
+        if t: scores()
+        tt(r("SB1"), r("PA", 0, C), r("MX"), OP.min)
+        do("V", lambda e: e.tensor_tensor_scan(ap(r("ST")), ap(r("NX")), ap(r("SB1")), 0.0, OP.add, OP.max), [r("NX"), r("SB1")], [r("ST")])
+        ts(r("NS"), r("ST", 15, C, 16), -1.0, OP.mult)
+        if t == 0: setup_first()
+        fq = [(A, b) for A in range(4) for b in range(4)]
+        if t == 0: setup_moves()
+        for j in range(6):
+            for a in range(24 - SSHARE, 24) if j == FFIRST else ():
+                m = 16 * a + 16
+                x, y = r("TM", C * (a % 2), C * (a % 2) + m), r("C%d" % (a // 4 - 2), a % 4, 4 * m, 4)
+                src, b = r("TS", 0, m), r("NS", a, a + 1)
+                do("S", lambda e: e.activation(ap(x), ap(src), ActivationFunctionType.Relu, bias=ap(b)), [src, b], [x])
+                do("S", lambda e: e.activation(ap(y), ap(x), ActivationFunctionType.Sign), [x], [y])
+            n = "C%d" % (j % 2 if j < 4 else j - 2)
+            for e in range(4):
+                a = 4 * j + e
+                m = 16 * a + 16
+                col = r("ST", m - 1, m)
+                if a < 24 - SSHARE: ts(r(n, e, 4 * m, 4), r("TS", 0, m), col, OP.is_gt)
+                if m < C: ts(r(n, 4 * m + e, 4 * C, 4), r("TS", m, C), col, OP.is_ge)
+            quant("QT", C * j, C * j + C, r(n))
+            mm("PB", K("gone"), ("QT", C * j), C, j == 0, j == 5)
+            if j == 4:
+                tt(r("ET", 0, 4 * C, 4), r("PA", 0, C), r("ST"), OP.is_equal)
+                quant("QT", 6 * C, 7 * C, r("ET"))
+                mm("PB", K("gone"), ("QT", 6 * C), C, False, False)
+            if t and j == 1:
+                quant("QIN", 0, 128, r("IN"))
+                inject(True)
+            for _ in range(3):
+                if fq and j < 6:
+                    A, b = fq.pop(0)
+                    bk = ("PCC", "PD")[rot[0] % 2]
+                    rot[0] += 1
+                    mm(bk, ("QF", 512 * A + 128 * b), ("QX", 0), C)
+                    act(r("FT", 1536 * b + C * A, 1536 * b + C * A + C), r(bk, 0, C), scale=0.5)
+        if t == 0: quant_tiles("qsel", "own2")
+        ts(r("GT", 0, C), r("PB", 0, C), float(GW + 1), OP.is_lt)
+        quant("QG", 0, 128, r("GT"))
+        mm("PA", K("qsel"), ("QG", 0), 128)
+        if t == 0:
+            tc(r("LW"), r("IJF"))
+            tt(r("ML"), r("IJF"), r("LW"), OP.is_lt, off=r("OFJ", 0, 24))
+            for k in range(3):
+                of = r("OFT", 24 * k, 24 * k + 24)
+                le = ("LE", "LT", "EQ")[k]
+                tt(r(le), r("TS"), r("NB", 0, C), OP.is_equal, off=of)
+                if k == 0: tt(r("RF", 0, C), r(le), r("ML"), OP.mult)
+                else: act(r("RF", C * k, C * k + C), r(le), scale=P("g0" if k == 1 else "g2"))
+                tt(r("AW", C * k, C * k + C), r("TS"), r("NB", 0, C), OP.is_lt, off=of)
+            quant("QAW", 0, 320, r("AW"))
+            quant("QRF", 0, 320, r("RF"))
+            for k in range(3):
+                for j, n in enumerate(("QAW", "QRF")): mm("PV%d" % k, K("q3"), (n, 96 * k), 128, j == 0, j == 1)
+            for k in range(3):
+                for j, n in enumerate(("QAW", "QRF")): mm("PV3", K("q1_%d" % k), (n, 96 * k), 128, k == 0 and j == 0, k == 2 and j == 1)
+        ts(r("G3"), r("PA", 0, 96), 6.0, OP.mult, -3.0, OP.add)
+        ts(r("G9"), r("PA", 0, 96), 9.0, OP.mult, 0.5, OP.add)
+
+        def aux_list():
+            tt(r("SB2"), r("PB", 0, C), r("MD"), OP.mult)
+            scan(r("ST2"), r("ND"), r("SB2"))
+            ts(r("PLo"), r("ST2", 15, C, 16), -1.0, OP.add)
+            o = r("PLo")
+            do("V", lambda e: e.tensor_copy(T.LW[:, 0:C].indirect(ap(o)), ap(r("IJF"))), [r("IJF"), o], [r("LW")])
+
+        def list2():
+            tt(r("SB3"), r("LW", 0, GW), r("MD", 0, GW), OP.mult)
+            scan(r("ST3"), r("ND", 0, GW), r("SB3"))
+            ts(r("ELo"), r("ST3", 15, GW, 16), P("A384"), OP.add)
+
+        def gates():
+            for b in range(4):
+                act(r("E%d" % t, b, 4 * GW, 4), r("FT", 1536 * b, 1536 * b + 1536), scale=2.0, off=r("ELo"))
+
+        def pass_on():
+            quant("QE", 128 * t, 128 * t + 128, r("E%d" % t))
+            send(t)
+
+        def scores_at(k):
+            return lambda: act(r("NB", C * k, C * k + C), r("TS"), off=r("OFT", 24 * k, 24 * k + 24))
+
+        def order(j):
+            a, b = ((0, 1), (0, 2), (1, 2))[j]
+            return lambda: tt(r("RF", C * j, C * j + C), r("TS"), r("NB", C * a, C * a + C), OP.is_lt, off=r("OFT", 24 * b, 24 * b + 24))
+
+        def orders():
+            order(2)()
+            quant("QRF", 0, 320, r("RF"))
+            for j, (bk, a, ka, b, kb) in enumerate((("PA", 0, "qneg", 1, "qneg"), ("PB", 0, "qsel", 2, "qneg"))):
+                mm(bk, K(ka), ("QRF", 96 * a), 128, True, False)
+                mm(bk, K(kb), ("QRF", 96 * b), 128, False, True)
+
+        def orders2():
+            for j, bk in enumerate(("PA", "PB")): act(r("R%d" % j), r(bk, 0, 96), bias=3.0 - j)
+            mm("PA", K("qsel"), ("QRF", 96), 128, True, False)
+            mm("PA", K("qsel"), ("QRF", 192), 128, False, True)
+            act(r("R2"), r("PA", 0, 96), bias=1.0)
+
+        def slots(n):
+            for _ in range(n):
+                if not sq: return
+                A, j = sq.pop(0)
+                mm("PCC" if A % 2 == 0 else "PD", K("cls%d" % A), ("QT", C * (6 if j == 0 else j - 1)), C, j == 0, j == 6)
+                if j == 6: pend.append(A)
+
+        def slot_copies():
+            while pend:
+                A = pend.pop(0)
+                act(r("SL", C * A, C * A + C), r("PCC" if A % 2 == 0 else "PD", 0, C), bias=float(C * A - 1))
+
+        sq = [(A, j) for A in range(4) for j in range(7)]
+        pend = []
+        onS = [[scores_at(0)], [scores_at(1)], [gates], [], [], [orders2]]
+        onV = [[aux_list], [list2], [order(0)], [pass_on, order(1)], [orders], []]
+        if t == 0:
+            setup_classes()
+            onS[1].append(setup_hops)
+            onV[0].append(lambda: quant_tiles("cls0", "cls3"))
+            onV[0].append(setup_routes)
+            onV[2].append(lambda: quant_tiles("hop0", "hop2"))
+            onV[2].append(lambda: quant_tiles("hopf0", "gb"))
+            for k in range(3): onV[2 + k].append(lambda k=k: setup_ends(k))
+            onV[5].append(setup_layer)
+        for i in range(SWEEPS):
+            tt(r("MA"), r("PV0", 0, 96), r("G3"), OP.max)
+            tt(r("MB"), r("PV1", 0, 96), r("MA"), OP.max)
+            tt(r("MC"), r("PV2", 0, 96), r("MB"), OP.max)
+            tt(r("TU"), r("PV3", 0, 96), r("MC"), OP.is_ge)
+            if t == 0 or i: state()
+            masked(r("TU"))
+            ts(r("IN", 0, 4 * 96, 4), r("MC"), -1.0 / 3.0, OP.mult, 1.0, OP.add)
+            quant("QIN", 0, 128, r("IN"))
+            gather_w(VSWEEP[i])
+            slot_copies()
+            for f in onS[i]: f()
+            inject(False)
+            for f in onV[i]: f()
+            quant("QGA", 0, 288, r("GA", 0, 1152))
+            for k in range(3): mm("PV%d" % k, K("came%d" % k), ("QGA", 96 * k), 128, False, True)
+            for k in range(3): mm("PV3", K("own%d" % k), ("QGA", 96 * k), 128, False, k == 2)
+            slots(SLOTS[i])
+        for k in range(3): tt(r("va%d" % k), r("PV%d" % k, 0, 96), r("R%d" % k), OP.min)
+        if t < R - 1:
+            state()
+            act(r("IN", 0, 4 * 96, 4), r("PV0", 0, 96), scale=0.0)
+        else:
+            ts(r("ba"), r("PV3", 0, 96), 1.0, OP.is_ge, P("bit"), OP.mult)
+            ts(r("bb"), r("PV3", 0, 96), -1.0, OP.is_le, P("bit8"), OP.mult)
+        for k in range(3): tt(r("mx%d" % k), r("va%d" % k), r("G9") if k == 0 else r("mx%d" % (k - 1)), OP.max)
+        for k in range(3): tt(r("pk%d" % k), r("va%d" % k), r("mx2"), OP.is_ge)
+        tt(r("self"), r("mx2"), r("G9"), OP.is_equal)
+        tt(r("SJ"), r("self"), r("JC"), OP.mult)
+        for k in range(3): tt(r("t%d" % k), r("pk%d" % k), r("OC%d" % k), OP.mult)
+        tt(r("ua"), r("t0"), r("SJ"), OP.add)
+        tt(r("ub"), r("t1"), r("t2"), OP.add)
+        tt(r("PP"), r("ua"), r("ub"), OP.add)
+        masked(r("PP"))
+        for h in range(3):
+            last = h == 2
+            gather_w(VHOP)
+            slot_copies()
+            if h == 0:
+                quant("QW", 0, 128, r("W"))
+                mm("PV3", K("hopf0"), ("QW", 0), 128)
+            else:
+                for b in (2 * h - 2, 2 * h - 1):
+                    act(r("FD", C * b, C * b + C), r("FT", 1536 * b, 1536 * b + 1536), off=r("DL"))
+            quant("QGA", 0, 288, r("GA", 0, 1152))
+            for k in range(3): mm(("PA", "PB", "PV2")[k], K("hop%s%d" % ("f" if last else "", k)), ("QGA", 96 * k), 128)
+            slots(SLOTS[SWEEPS + h])
+            if h == 0:
+                to_list(r("PV3", 0, 96), r("DL"))
+                tt(r("SJF"), r("self"), r("JF"), OP.mult)
+            if last:
+                a, o = (0, 0) if t == 0 else (GW * t, 32)
+                for j in range(8):
+                    two = [("PV0", "PV1", "PV3", "PD")[2 * (j % 2) + i] for i in range(2)]
+                    for i in range(2): mm(two[i], ("WP", 256 * j + 128 * i), ("LD", a), 128)
+                    for i in range(2):
+                        b, A = j // 2, 2 * (j % 2) + i
+                        act(r("HT", 1536 * b + C * A, 1536 * b + C * A + GW), r(two[i], o, o + GW), scale=0.015625)
+            for k in range(3): tt(r("t%d" % k), r(("PA", "PB", "PV2")[k], 0, 96), r("pk%d" % k), OP.mult)
+            tt(r("ua"), r("t0"), r("SJF") if last else r("SJ"), OP.add)
+            tt(r("ub"), r("t1"), r("t2"), OP.add)
+            if last:
+                tt(r("PE"), r("ua"), r("ub"), OP.add)
+            else:
+                tt(r("PP"), r("ua"), r("ub"), OP.add)
+                masked(r("PP"))
+        to_list(r("PE"), r("EL"))
+        if t == R - 1: number_parts()
+        tt(r("SB2"), r("SL"), r("MD"), OP.mult, off=r("EL"))
+        scan(r("ST2"), r("ND"), r("SB2"))
+        tc(r("HL"), r("ST2", 15, C, 16))
+        for b in range(4):
+            tt(r("Z", C * b, C * b + C), r("FT", 1536 * b, 1536 * b + 1536), r("FD", C * b, C * b + C), OP.add, off=r("EL"))
+        xn = "X1"
+        for b in range(4):
+            tt(r(xn, b, 4 * C, 4), r("HT", 1536 * b, 1536 * b + 1536), r("Z", C * b, C * b + C), OP.add, off=r("HL"))
+        quant("QX", 0, C, r(xn))
+        if t == 0: quant("QV", 0, 128, r("VV"))
+    mm("PA", ("QV", 0), ("QX", 0), C)
+    act(r("TS", 2 * C, 3 * C), r("PA", 0, C))
+    dma("Y", "d7", [(T.oc[:], T.QXc[:, 0:C].bitcast(dt.uint8))] + [(T.osc[4 * k:4 * k + 4, :], T.QXs[32 * k:32 * k + 4, 0:C]) for k in range(4)], rd=[r("QXc"), r("QXs")])
+    dma("Y", "d8", [(T.y[:], T.TS[:, 2 * C:3 * C])], rd=[r("TS", 2 * C, 3 * C)])
+    quant("QND", 0, C, r("ET"))
+    mm("PB", K("ge"), ("QND", 0), C, True, False)
+    mm("PB", K("gm"), ("QND", 0), C, False, True)
+    mm("PCC", K("gb"), ("QND", 0), C)
+    act(r("TS", 0, C), r("PB", 0, C))
+    act(r("TS", C, 2 * C), r("PCC", 0, C))
+    dma("Y", "d9", [(T.nd[:], T.TS[0:128:16, 0:2 * C])], rd=[r("TS", 0, 2 * C)])
+    for s in SEMAPHORES:
+        if cnt[s]: g.wait_ge(T.sem[s], cnt[s])

@@ -3,25 +3,26 @@ from concourse.bass import DstId, RemoteDMATransfer
 from concourse.mybir import dt, AluOpType, AxisListType, ActivationFunctionType
 
 OP = AluOpType
-COPY = ActivationFunctionType.Copy
+COPY, IDENT = ActivationFunctionType.Copy, ActivationFunctionType.Identity
 C, GW, R, SWEEPS = 384, 96, 3, 6
 JUMP = [0, 1, 4]
 
 TILES = ["gone", "qsel", "qneg", "q3", "q1_0", "q1_1", "q1_2", "st0", "st1", "st2", "sto", "came0", "came1", "came2",
-         "own0", "own1", "own2", "hop0", "hop1", "hop2", "cls0", "cls1", "cls2", "cls3", "hopf0", "hopf1", "hopf2", "ge", "gm", "gb"]
+         "own0", "own1", "own2", "hop0", "hop1", "hop2", "cls0", "cls1", "cls2", "cls3", "hopf0", "ct0", "ct1", "ct2", "ct3", "ge", "gm", "gb"]
 TI = {n: i for i, n in enumerate(TILES)}
 NT = len(TILES)
 VSWEEP = [0, 448, 352, 320, 224, 512]
 VHOP = 512
-SLOTS = [3, 3, 3, 3, 3, 3, 4, 6, 0]
-FFIRST = 3
-SSHARE = 0
+SLOTS = [4, 4, 4, 4, 4, 4, 4]
+FSHARE = [6, 4, 3, 3, 0, 0]
+FFIRST = 2
+SSHARE = 3
 ENGINES = 8
 
 F32, BF, I32, U16, X4, U8 = "float32", "bfloat16", "int32", "uint16", "float8_e4m3fn_x4", "uint8"
 SCRATCH = {}
-WIDE = {"KF": "JM MD ND IJF CMr RM J4 J0 J1 J2 D0 D1 D2", "KI": "PC UL WL", "XI": "EI EP",
-        "XF": "SB1 ST SB2 ST2 SB3 ST3 t0 t1 t2 ua ub PE la lb lc qa qb qd qm JF SJF ea eb ec ba bb",
+WIDE = {"KF": "JM MD ND IJF CMr RM J0 J1 J2 D0 D1 D2", "KI": "PC UL WL", "XI": "EI EP",
+        "XF": "SB1 ST SB2 ST2 SB3 ST3 t0 t1 t2 ua ub PE la lb lc qa qb qd qm ea eb ec ba bb",
         "XB": "G3 G9 MA MB MC TU R0 R1 R2 va0 va1 va2 mx0 mx1 mx2 pk0 pk1 pk2 self SJ PP OC0 OC1 OC2 JC EQ LT LE ML"}
 HOME = {n: w for w in WIDE for n in WIDE[w].split()}
 PLACE, LEN = {}, {}
@@ -40,43 +41,38 @@ def mx(name, n):
 
 
 for _n, _w, _d in [
-        ("X0", 1536, BF), ("X1", 1536, BF), ("U", 512, BF), ("VV", 512, BF),
+        ("X0", 1536, BF), ("U", 512, BF), ("VV", 512, BF),
         ("LKT", 72, I32), ("LKS", 72, I32), ("OFT", 72, U16), ("OFJ", 72, U16), ("OFS", 72, U16),
         ("UL", 24, I32), ("ULo", 24, U16), ("WL", 128, I32), ("WLo", 128, U16),
         ("PC", 16, I32), ("PF", 48, F32), ("WT", 1024, BF), ("CB", 512 * NT, BF), ("FB", 4 * 516, BF),
-        ("GC", 96, BF), ("GCt", 96, BF), ("GOt", 512, BF),
+        ("GC", 96, BF), ("GCt", 96, BF), ("GD", 128, BF), ("GDt", 128, BF), ("GH", 96, BF), ("KM", 32, BF), ("GOt", 512, BF),
         ("JM", C, F32), ("MD", C, F32), ("ND", C, F32), ("MX", C, F32), ("NX", C, F32), ("NS", 24, F32), ("TM", 2 * C, BF), ("IJF", C, F32),
-        ("CMr", 96, F32), ("RM", 96, F32), ("J4", 96, F32), ("J0", 96, F32), ("J1", 96, F32), ("J2", 96, F32), ("KM", 32, BF), ("GH", 96, BF), ("qm", C, F32),
+        ("CMr", 96, F32), ("RM", 96, F32), ("J0", 96, F32), ("J1", 96, F32), ("J2", 96, F32), ("qm", C, F32),
         ("TS", 3 * C, F32), ("SB1", C, F32), ("ST", C, F32), ("EQ", C, BF), ("ET", 4 * C, BF),
         ("GT", 512, BF), ("G3", 96, BF), ("G9", 96, BF), ("PLo", 24, U16), ("LW", C, F32), ("SB2", C, F32),
         ("ST2", C, F32), ("SB3", GW, F32), ("ST3", GW, F32), ("ELo", 6, U16),
-        ("FT", 16 * C, BF), ("HT", 16 * C, BF), ("SL", 4 * C, F32), ("FD", 4 * C, BF), ("Z", 4 * C, BF),
+        ("FT", 16 * C, BF), ("HT", 16 * C, BF), ("SL", 4 * C, F32), ("FD", 4 * C, BF), ("Z", 4 * C, BF), ("WA", 4 * C, BF),
         ("LT", C, BF), ("LE", C, BF), ("ML", C, BF), ("AW", 1280, BF), ("RF", 1280, BF), ("NB", 2 * C, F32),
         ("MA", 96, BF), ("MB", 96, BF), ("MC", 96, BF), ("IN", 512, BF), ("TU", 96, BF), ("W", 512, BF), ("GA", 1280, BF),
         ("R0", 96, BF), ("R1", 96, BF), ("R2", 96, BF), ("va0", 96, BF), ("va1", 96, BF), ("va2", 96, BF),
         ("mx0", 96, BF), ("mx1", 96, BF), ("mx2", 96, BF), ("pk0", 96, BF), ("pk1", 96, BF), ("pk2", 96, BF),
-        ("self", 96, BF), ("SJ", 96, BF), ("SJF", 96, F32), ("t0", 96, F32), ("t1", 96, F32), ("t2", 96, F32),
+        ("self", 96, BF), ("SJ", 96, BF), ("t0", 96, F32), ("t1", 96, F32), ("t2", 96, F32),
         ("ua", 96, F32), ("ub", 96, F32), ("PP", 96, BF), ("PE", 96, F32),
         ("la", 96, F32), ("lb", 48, F32), ("lc", 24, F32), ("DL", 24, U16), ("EL", 24, U16), ("HL", 24, U16),
         ("D0", C, F32), ("D1", C, F32), ("D2", C, F32), ("CTF", C, F32),
-        ("qa", C, F32), ("qb", 192, F32), ("qd", 96, F32), ("OC0", 96, BF), ("OC1", 96, BF), ("OC2", 96, BF), ("JC", 96, BF), ("JF", 96, F32),
+        ("qa", C, F32), ("qb", 192, F32), ("qd", 96, F32), ("OC0", 96, BF), ("OC1", 96, BF), ("OC2", 96, BF), ("JC", 96, BF),
         ("ea", 96, F32), ("eb", 96, F32), ("ec", 96, F32), ("EI", 96, I32), ("EP", 288, I32), ("ba", 96, F32), ("bb", 96, F32),
-        ]:
+        ("C0", 4 * C, BF), ("C1", 4 * C, BF), ("C2", 4 * C, BF), ("E0", 512, BF), ("E1", 512, BF), ("E2", 512, BF)]:
     sb(_n, _w, _d)
 for _n, _w in [("QX", C), ("QU", 128), ("QUP", C), ("QV", 128), ("WC", 512), ("WP", 2048), ("QK", 128 * NT), ("QF", 2048),
                ("QT", 7 * C), ("QG", 128), ("QAW", 320), ("QRF", 320), ("QIN", 128), ("QGA", 320), ("QW", 128),
                ("QE", 3 * 128), ("LD", 320), ("QND", C)]:
     mx(_n, _w)
-for _i in range(7):
-    if _i < 4:
-        sb("C%d" % _i, 4 * C, BF)
-for _i in range(R):
-    sb("E%d" % _i, 512, BF)
 PS = ["PV0", "PV1", "PV2", "PV3", "PA", "PB", "PCC", "PD"]
 for _n in PS:
     SCRATCH[_n] = ("psum", [128, 512], F32)
     PLACE[_n], LEN[_n] = (_n, 0), 512
-SEMAPHORES = ["sv", "ss", "st", "sg", "lcl", "arr0", "arr1", "arr2"] + ["d%d" % i for i in range(16)]
+SEMAPHORES = ["sv", "ss", "st", "sg", "lcl", "arr0", "arr1", "arr2"] + ["d%d" % i for i in range(10)]
 
 
 def rank_program(g, core, T, topo):
@@ -184,13 +180,13 @@ def rank_program(g, core, T, topo):
         if off is None: do("V", lambda e: e.tensor_copy(ap(o), ap(a)), [a], [o])
         else: do("V", lambda e: e.tensor_copy(ap(o), ap(a).indirect(ap(off))), [a, off], [o])
 
-    def act(o, a, bias=0.0, scale=1.0, off=None):
-        rd = [a] + [x for x in (scale, off) if isr(x)]
-        if off is None: do("S", lambda e: e.activation(ap(o), ap(a), COPY, bias=bias, scale=val(scale)), rd, [o])
-        else: do("S", lambda e: e.activation(ap(o), ap(a).indirect(ap(off)), COPY, bias=bias, scale=val(scale)), rd, [o])
+    def act(o, a, bias=0.0, scale=1.0, off=None, fn=COPY):
+        rd = [a] + [x for x in (scale, bias, off) if isr(x)]
+        if off is None: do("S", lambda e: e.activation(ap(o), ap(a), fn, bias=val(bias), scale=val(scale)), rd, [o])
+        else: do("S", lambda e: e.activation(ap(o), ap(a).indirect(ap(off)), fn, bias=val(bias), scale=val(scale)), rd, [o])
 
-    def scan(o, a, b):
-        do("V", lambda e: e.tensor_tensor_scan(ap(o), ap(a), ap(b), 0.0, OP.mult, OP.add), [a, b], [o])
+    def scan(o, a, b, op0=OP.mult, op1=OP.add):
+        do("V", lambda e: e.tensor_tensor_scan(ap(o), ap(a), ap(b), 0.0, op0, op1), [a, b], [o])
 
     def fill(o, c):
         do("V", lambda e: e.memset(ap(o), c), [], [o])
@@ -198,6 +194,11 @@ def rank_program(g, core, T, topo):
     def quant(n, a, b, src):
         q, s = r(n + "c", a, b), r(n + "s", a, b)
         do("V", lambda e: e.quantize_mx(ap(q), ap(s), ap(src)), [src], [q, s])
+
+    def pick(n, src, k, off):
+        m, w = 16 * (off[2] - off[1]), LEN[src + "c"]
+        do("V", lambda e: e.tensor_copy(T[n + "c"][:, 0:m].bitcast(dt.uint32), T[src + "c"][:, 0:w].bitcast(dt.uint32).indirect(ap(off))), [r(src + "c"), off], [r(n + "c")])
+        do("S", lambda e: e.activation(T[n + "s"][:, 0:m], T[src + "s"][:, 0:w].indirect(ap(off)), COPY), [r(src + "s"), off], [r(n + "s")])
 
     def mm(bk, st, mv, n, start=True, stop=True):
         l, ls = r(st[0] + "c", st[1], st[1] + 128), r(st[0] + "s", st[1], st[1] + 128)
@@ -215,6 +216,7 @@ def rank_program(g, core, T, topo):
 
     K = lambda n: ("QK", 128 * TI[n])
     tile0 = lambda n: 512 * TI[n]
+    tile = lambda n, a=0, st=1: r("CB", tile0(n) + a, tile0(n) + 512, st)
 
     dma("Y", "d0", [(T.X0[:], T.x[:])], wr=[r("X0")])
     dma("S", "d1", [(T.U[:], T.u[:])], wr=[r("U")])
@@ -231,6 +233,7 @@ def rank_program(g, core, T, topo):
     dma("Y", "d5", [(T.VV[:], T.v[:])], wr=[r("VV")])
 
     GRP = {0: ([[16, 8]], 0), 1: ([[32, 4], [-16, 2]], 16), 4: ([[-64, 2], [16, 4]], 64)}
+    CLS = lambda A: 16 * (A & 1) + 64 * (A >> 1)
     neg = lambda pat: [[-a, b] for a, b in pat]
     for k in range(3):
         iota(r("UL", 8 * k, 8 * k + 8), GRP[JUMP[k]][0], GRP[JUMP[k]][1], 0)
@@ -241,7 +244,8 @@ def rank_program(g, core, T, topo):
         fill(r("WT", 512 + 128 * j, 640 + 128 * j), w)
     WCOL = {1.0: 0, -6.0: 512, -2.0: 640, 3.0: 768, -1.0: 896}
     tc(r("ULo"), r("UL"))
-    fill(r("FB"), 0.0)
+    for a in (0, 1024): act(r("FB", a, a + 1024), r("WT", 0, 1024), scale=0.0)
+    act(r("FB", 2048), r("WT", 0, 16), scale=0.0)
     PFC = {}
 
     def pcol(name):
@@ -249,36 +253,41 @@ def rank_program(g, core, T, topo):
         return r("PF", PFC[name], PFC[name] + 1)
 
     P = lambda name: r("PF", PFC[name], PFC[name] + 1)
+
+    def scol(name, a, scale=1.0, bias=0.0):
+        act(pcol(name), P(a), bias=bias, scale=scale, fn=IDENT if isr(bias) else COPY)
+
     p = r("PC", 0, 1)
     for j, (n, sh, an) in enumerate([("i", 0, 15), ("s", 0, 3), ("kk", 2, 3), ("g0", 4, 1), ("g1", 5, 1), ("g2", 6, 1)]):
         o = r("PC", j + 1, j + 2)
         ts(o, p, sh, OP.arith_shift_right, an, OP.bitwise_and)
         tc(pcol(n), o)
     ts(r("MD"), r("JM"), P("i"), OP.is_equal)
-    ts(r("ND"), r("JM"), P("i"), OP.not_equal)
-    ts(r("MX"), r("MD"), 2e29, OP.mult, -1e29, OP.add)
+    act(r("MX"), r("MD"), scale=2e29, bias=-1e29)
+    act(r("ND"), r("MD"), scale=-1.0, bias=1.0)
     act(r("NX"), r("MD"), scale=-2e29)
     for A in range(4):
         for h in range(2):
             a = 516 * A + 3 + 256 * h
-            sel(r("FB", a, a + 253, 4), r("WT", 0, 64), [[-32, 2], [0, 2], [-1, 16]], OP.is_equal, 0.0, -(16 * (A & 1) + 64 * (A >> 1)), 1)
+            sel(r("FB", a, a + 253, 4), r("WT", 0, 64), [[-32, 2], [0, 2], [-1, 16]], OP.is_equal, 0.0, -CLS(A), 1)
+    for k in range(3):
+        gp, gb = GRP[JUMP[k]]
+        sel(r("GCt", 32 * k, 32 * k + 32), r("WT", 0, 32), neg(gp) + [[0, 4]], OP.is_ge, 0.0, -gb, 1)
+        sel(r("GC", 32 * k, 32 * k + 32), r("GCt", 32 * k, 32 * k + 32), gp + [[0, 4]], OP.is_ge, 0.0, gb + 15, -1)
     sel(r("NX"), r("NX"), [[0, 24], [1, 16]], OP.not_equal, -2e29, 0, 0)
-    t0 = tile0("gone")
     sel(r("GOt"), r("WT", 0, 512), [[-16, 8], [0, 64]], OP.is_ge, 0.0, 0, 1)
-    sel(r("CB", t0, t0 + 512), r("GOt"), [[16, 8], [0, 64]], OP.is_ge, 0.0, 15, -1)
-    quant("QU", 0, 128, r("U"))
-    off = r("ULo")
-    do("V", lambda e: e.tensor_copy(T.QUPc[:, 0:384].bitcast(dt.uint32), T.QUc[:, 0:128].bitcast(dt.uint32).indirect(ap(off))), [r("QUc"), off], [r("QUPc")])
+    sel(tile("gone"), r("GOt"), [[16, 8], [0, 64]], OP.is_ge, 0.0, 15, -1)
+
     def zeros(a, b):
         while a < b:
             n = min(1024, b - a)
             act(r("CB", a, a + n), r("WT", 0, n), scale=0.0)
             a += n
 
-    zc = tile0("came0")
+    z0, zc = tile0("qsel"), tile0("came0")
+    quant("QU", 0, 128, r("U"))
     zeros(zc, zc + 2048)
-    do("S", lambda e: e.activation(T.QUPs[:, 0:384], T.QUs[:, 0:128].indirect(ap(off)), COPY), [r("QUs"), off], [r("QUPs")])
-    z0 = tile0("qsel")
+    pick("QUP", "QU", 3, r("ULo"))
     quant("QX", 0, C, r("X0"))
 
     def scores():
@@ -292,64 +301,60 @@ def rank_program(g, core, T, topo):
 
     scores()
     act(r("NB", 0, C), r("PB", 0, C))
+    for k, n in ((1, "g0"), (2, "g2")): scol("sg%d" % k, n, -2.0, 1.0)
+    act(r("NB", C, 2 * C), r("PB", 0, C), scale=P("sg1"))
+    act(r("SB2"), r("PB", 0, C), scale=P("sg2"))
+    act(r("SL", 0, C), r("PCC", 0, C), scale=P("sg1"))
+    act(r("SL", C, 2 * C), r("PD", 0, C), scale=P("sg2"))
+    act(r("RF", C, 512), r("WT", 0, 512 - C), scale=0.0)
 
     def setup_first():
-        quant("QK", 0, 128, r("CB", 0, 512))
+        quant("QK", 0, 128, tile("gone"))
         for A in range(4):
             for b in range(4):
                 quant("QF", 512 * A + 128 * b, 512 * A + 128 * b + 128, r("FB", 516 * A + 3 - b, 516 * A + 515 - b))
 
-    zeros(z0, zc)
-    zeros(zc + 2048, tile0("cls0"))
-    for a in (0, 768): act(r("ET", a, a + 768), r("WT", 0, 768), scale=0.0)
+    fill(r("CB", z0, zc), 0.0)
     for n, a in (("GT", C), ("W", C), ("GA", 1152), ("AW", 1152), ("RF", 1152)):
         fill(r(n, a), 0.0)
     for t in range(R):
         fill(r("E%d" % t, 4 * GW, 512), 0.0)
-    fill(r("IN"), 0.0)
-    fill(r("GA", 640, 1152), 0.0)
-    quant("QGA", 192, 320, r("GA", 768, 1280))
+
+    def setup_zeros():
+        zeros(zc + 2048, tile0("hop0"))
+        for a in (0, 768): act(r("ET", a, a + 768), r("WT", 0, 768), scale=0.0)
+        act(r("IN"), r("WT", 0, 512), scale=0.0)
+        act(r("GA", 640, 1152), r("WT", 0, 512), scale=0.0)
+
     iota(r("IJF"), [[1, C]], 0, 0)
-
-    def stile(n, c, pat, base, w):
-        gp, gb = GRP[c]
+    for n, w in (("qsel", 1.0), ("qneg", -1.0), ("q3", 3.0)):
         for s in range(4):
-            a = tile0(n) + 5 * s
-            o = r("CB", a, tile0(n) + 512, 16)
-            sel(o, r("WT", WCOL[w], WCOL[w] + 32), neg(gp) + pat, OP.is_equal, 0.0, -gb - base - s, 1)
-
-    def otile(n, c, k, w):
-        gp, gb = GRP[c]
+            sel(tile(n, 5 * s, 16), r("WT", WCOL[w], WCOL[w] + 32), [[-16, 8], [-4, 4]], OP.is_equal, 0.0, -s, 1)
+    for k in range(3):
         for s in range(4):
-            o = r("CB", tile0(n) + 16 * k + 5 * s, tile0(n) + 512, 64)
-            sel(o, r("WT", WCOL[w], WCOL[w] + 8), neg(gp), OP.is_equal, 0.0, -gb - 4 * k - s, 1)
-
-    stile("qsel", 0, [[-4, 4]], 0, 1.0)
-    stile("qneg", 0, [[-4, 4]], 0, -1.0)
-    stile("q3", 0, [[-4, 4]], 0, 3.0)
-    for k in range(3): otile("q1_%d" % k, 0, k, 1.0)
+            sel(tile("q1_%d" % k, 16 * k + 5 * s, 64), r("WT", 0, 8), [[-16, 8]], OP.is_equal, 0.0, -4 * k - s, 1)
     for k in range(3):
-        for e in (0, 1 + k): sel(r("CB", tile0("st%d" % k) + e, tile0("st%d" % k) + 512, 4), r("WT", WCOL[3.0], WCOL[3.0] + 128), [[-1, 128]], OP.is_equal, 0.0, 0, 1)
-    sel(r("CB", tile0("sto"), tile0("sto") + 512, 4), r("WT", 0, 128), [[-1, 128]], OP.is_equal, 0.0, 0, 1)
+        for e in (0, 1 + k): sel(tile("st%d" % k, e, 4), r("WT", WCOL[3.0], WCOL[3.0] + 128), [[-1, 128]], OP.is_equal, 0.0, 0, 1)
+    sel(tile("sto", 0, 4), r("WT", 0, 128), [[-1, 128]], OP.is_equal, 0.0, 0, 1)
     for k in range(3):
-        for s in range(4): sel(r("CB", tile0("sto") + 16 * k + 4 * s + 1 + k, tile0("sto") + 512, 64), r("WT", 0, 8), [[-16, 8]], OP.is_equal, 0.0, -4 * k - s, 1)
-    for k in range(3):
-        gp, gb = GRP[JUMP[k]]
-        sel(r("GCt", 32 * k, 32 * k + 32), r("WT", 0, 32), neg(gp) + [[0, 4]], OP.is_ge, 0.0, -gb, 1)
-        sel(r("GC", 32 * k, 32 * k + 32), r("GCt", 32 * k, 32 * k + 32), gp + [[0, 4]], OP.is_ge, 0.0, gb + 15, -1)
+        for s in range(4): sel(tile("sto", 16 * k + 4 * s + 1 + k, 64), r("WT", 0, 8), [[-16, 8]], OP.is_equal, 0.0, -4 * k - s, 1)
+    for A in range(4):
+        a = 32 * A
+        sel(r("GDt", a, a + 32), r("WT", 0, 32), [[0, 2], [-32, 2], [0, 8]], OP.is_ge, 0.0, -CLS(A), 1)
+        sel(r("GD", a, a + 32), r("GDt", a, a + 32), [[0, 2], [32, 2], [0, 8]], OP.is_ge, 0.0, CLS(A) + 15, -1)
     iota(r("CMr"), [[0, 24], [1, 4]], 0, 0)
     iota(r("D0"), [[0, 48], [1, 8]], 0, 0)
     iota(r("D1"), [[0, 6], [8, 8], [0, 8]], 0, 0)
     iota(r("D2"), [[64, 6], [0, 64]], 0, 0)
-    iota(r("J4"), [[4, 96]], 0, 0)
     iota(r("J0"), [[0, 48], [4, 2]], 0, 0)
     iota(r("J1"), [[0, 6], [8, 8], [0, 2]], 0, 0)
     iota(r("J2"), [[64, 6], [0, 16]], 0, 0)
+    iota(r("CB", tile0("hop0"), tile0("cls0")), [[0, 1536]], 0, 0)
     iota(r("CB", tile0("hopf0"), tile0("gb") + 512), [[0, 512 * (TI["gb"] + 1 - TI["hopf0"])]], 0, 0)
     for b in range(4):
         for A in range(4):
             a = 32 * b + 8 * A
-            iota(r("WL", a, a + 8), [[0, 2], [32, 2], [0, 2]], 128 * b + 16 * (A & 1) + 64 * (A >> 1), 0)
+            iota(r("WL", a, a + 8), [[0, 2], [32, 2], [0, 2]], 128 * b + CLS(A), 0)
     iota(r("HT"), [[0, 16 * C]], 0, 0)
 
     def quant_tiles(a, b):
@@ -359,27 +364,35 @@ def rank_program(g, core, T, topo):
             quant("QK", 128 * a, 128 * (a + n), r("CB", 512 * a, 512 * (a + n)))
             a += n
 
-    def setup_lists():
-        tc(r("OFT", 0, 24), r("LKT", 0, 24))
-        for k in (1, 2): ts(r("OFT", 24 * k, 24 * k + 24), r("LKT", 24 * k, 24 * k + 24), float(C * k), OP.add)
-        tc(r("OFJ"), r("LKT"))
-        tc(r("OFS"), r("LKS"))
-        for s in range(4): ts(pcol("ms%d" % s), P("s"), float(s), OP.is_equal)
-        for k in range(4): ts(pcol("mr%d" % k), P("kk"), float(k), OP.is_equal)
+    tc(r("OFT", 0, 24), r("LKT", 0, 24))
+    for k in (1, 2): ts(r("OFT", 24 * k, 24 * k + 24), r("LKT", 24 * k, 24 * k + 24), float(C * k), OP.add)
+    tc(r("OFJ"), r("LKT"))
+    tc(r("OFS"), r("LKS"))
+    for s in range(4): ts(pcol("ms%d" % s), P("s"), float(s), OP.is_equal)
+    for k in range(4): ts(pcol("mr%d" % k), P("kk"), float(k), OP.is_equal)
+
+    def setup_columns():
         for k in range(3):
-            ts(pcol("mc%d" % k), P("mr%d" % k), -6.0, OP.mult)
-            ts(pcol("mw%d" % k), P("mr%d" % k), -2.0, OP.mult)
-        ts(pcol("A"), P("g2"), 2.0, OP.mult)
-        tt(pcol("A2"), P("A"), P("g0"), OP.add)
-        ts(pcol("A384"), P("A2"), 384.0, OP.mult)
+            scol("mc%d" % k, "mr%d" % k, -6.0)
+            scol("mw%d" % k, "mr%d" % k, -2.0)
+        scol("A2", "g2", 2.0, P("g0"))
+        scol("A384", "A2", 384.0)
+        scol("a3s", "A384", P("mr3"))
+        for k, n, f in ((1, "g0", 384.0), (2, "g2", 768.0)):
+            scol("x%d" % k, n, -2.0 * f, f)
+            scol("y%d" % k, "x%d" % k, 1.0, P("A384"))
+            scol("z%d" % k, "y%d" % k, P("mr3"))
+        scol("h768", "g1", 768.0)
+        scol("b1", "mr1", 2.0, P("mr0"))
+        scol("bit", "mr2", 4.0, P("b1"))
+        scol("bit8", "bit", 8.0)
+        for s in range(4): scol("mo%d" % s, "ms%d" % s, P("mr0"))
 
     def setup_moves():
         for k in range(3):
             for s in range(4):
-                a = tile0("came%d" % k)
-                act(r("CB", a + 5 * s, a + 512, 16), r("GC", 32 * k, 32 * k + 32), scale=P("mc%d" % k))
-                a = tile0("own%d" % k)
-                act(r("CB", a + 16 * k + 5 * s, a + 512, 64), r("GC", 32 * k + k, 32 * k + 32, 4), scale=P("mw%d" % k))
+                act(tile("came%d" % k, 5 * s, 16), r("GC", 32 * k, 32 * k + 32), scale=P("mc%d" % k))
+                act(tile("own%d" % k, 16 * k + 5 * s, 64), r("GC", 32 * k + k, 32 * k + 32, 4), scale=P("mw%d" % k))
 
     def setup_classes():
         for A in range(4):
@@ -387,59 +400,46 @@ def rank_program(g, core, T, topo):
                 o, src = tile0("cls%d" % A) + 128 * h, tile0("gone") + 64 * ((A & 1) + 2 * (h & 1) + 4 * (A >> 1))
                 for g0 in range(2): act(r("CB", o + 64 * g0, o + 64 * g0 + 64), r("CB", src, src + 64))
 
-    def setup_hops():
-        ts(r("KM"), r("CMr", 0, 32), P("kk"), OP.is_equal)
-        for k in range(3):
-            tt(r("GH", 32 * k, 32 * k + 32), r("GC", 32 * k, 32 * k + 32), r("KM"), OP.mult)
-            for s in range(4):
-                a = tile0("hop%d" % k) + 5 * s
-                act(r("CB", a, tile0("hop%d" % k) + 512, 16), r("GH", 32 * k, 32 * k + 32))
-                a = tile0("hopf%d" % k) + 5 * s
-                act(r("CB", a, tile0("hopf%d" % k) + 512, 16), r("GC", 32 * k, 32 * k + 32))
+    def setup_hops(k):
+        if k == 0: ts(r("KM"), r("CMr", 0, 32), P("kk"), OP.is_equal)
+        h = r("GH", 32 * k, 32 * k + 32)
+        tt(h, r("GC", 32 * k, 32 * k + 32), r("KM"), OP.mult)
+        for s in range(4): act(tile("hop%d" % k, 5 * s, 16), h)
+
+    def setup_tables():
+        for s in range(4): act(tile("hopf0", 5 * s, 16), r("GC", 0, 32))
+        for A in range(4):
+            d = r("GD", 32 * A, 32 * A + 32)
+            tt(d, d, r("KM"), OP.mult)
+            for s in range(4): act(tile("ct%d" % A, 5 * s, 16), d)
         for e, n in ((0, "ge"), (1, "ge"), (2, "gm"), (3, "gb")):
-            act(r("CB", tile0(n) + e, tile0(n) + 512, 4), r("CB", tile0("gone") + e, tile0("gone") + 512, 4))
+            act(tile(n, e, 4), tile("gone", e, 4))
 
     def setup_routes():
         ts(r("RM"), r("CMr"), P("kk"), OP.is_equal)
         for d in range(3): act(r("D%d" % d), r("D%d" % d), scale=P("mr%d" % d))
         tt(r("qa"), r("D0"), r("D1"), OP.add)
         tt(r("CTF"), r("qa"), r("D2"), OP.add)
-        tt(pcol("a3s"), P("A384"), P("mr3"), OP.mult)
-        for k, n, f in ((1, "g0", 384.0), (2, "g2", 768.0)):
-            ts(pcol("x%d" % k), P(n), -2.0 * f, OP.mult, f, OP.add)
-            tt(pcol("y%d" % k), P("x%d" % k), P("A384"), OP.add)
-            tt(pcol("z%d" % k), P("y%d" % k), P("mr3"), OP.mult)
-
-        ts(r("JF"), r("J4"), P("s"), OP.add, P("A384"), OP.add)
         ts(r("t0"), r("J0"), P("s"), OP.add, P("mr0"), OP.mult)
         ts(r("t1"), r("J1"), P("mr1"), OP.mult, P("a3s"), OP.add)
         ts(r("t2"), r("J2"), P("mr2"), OP.mult)
         tt(r("ua"), r("t0"), r("t1"), OP.add)
         tt(r("JC"), r("ua"), r("t2"), OP.add)
 
-    def setup_ends(k):
+    def setup_ends_s(k):
         act(r("qa"), r("CTF"), off=r("OFJ", 24 * k, 24 * k + 24))
         for s in range(4): act(r("qm", 96 * s, 96 * s + 96), r("qa", s, C, 4), scale=P("ms%d" % s))
+
+    def setup_ends(k):
         tt(r("qb"), r("qm", 0, 192), r("qm", 192, C), OP.add)
         tt(r("qd"), r("qb", 0, 96), r("qb", 96, 192), OP.add)
         ts(r("OC%d" % k), r("qd"), P("a3s") if k == 0 else P("z%d" % k), OP.add)
 
     def setup_layer():
         ts(r("WLo"), r("WL"), P("i"), OP.add)
-        wo = r("WLo")
-        do("V", lambda e: e.tensor_copy(T.WPc[:, 0:2048].bitcast(dt.uint32), T.WCc[:, 0:512].bitcast(dt.uint32).indirect(ap(wo))), [r("WCc"), wo], [r("WPc")])
-        do("S", lambda e: e.activation(T.WPs[:, 0:2048], T.WCs[:, 0:512].indirect(ap(wo)), COPY), [r("WCs"), wo], [r("WPs")])
+        pick("WP", "WC", 16, r("WLo"))
 
-    setup_lists()
-    ts(pcol("h768"), P("g1"), 768.0, OP.mult)
-    ts(pcol("two"), P("mr1"), 2.0, OP.mult)
-    ts(pcol("four"), P("mr2"), 4.0, OP.mult)
-    tt(pcol("six"), P("two"), P("four"), OP.add)
-    tt(pcol("bit"), P("six"), P("mr0"), OP.add)
-    ts(pcol("bit8"), P("bit"), 8.0, OP.mult)
-    for s in range(4): tt(pcol("mo%d" % s), P("ms%d" % s), P("mr0"), OP.mult)
-
-    def masked(src, wdt="W"):
+    def masked(src):
         for s in range(4):
             o = r("W", s, C, 4)
             if s < 2: ts(o, src, P("ms%d" % s), OP.mult)
@@ -497,24 +497,30 @@ def rank_program(g, core, T, topo):
     for t in range(R):
         if t: scores()
         tt(r("SB1"), r("PA", 0, C), r("MX"), OP.min)
-        do("V", lambda e: e.tensor_tensor_scan(ap(r("ST")), ap(r("NX")), ap(r("SB1")), 0.0, OP.add, OP.max), [r("NX"), r("SB1")], [r("ST")])
+        scan(r("ST"), r("NX"), r("SB1"), OP.add, OP.max)
         ts(r("NS"), r("ST", 15, C, 16), -1.0, OP.mult)
         if t == 0: setup_first()
         fq = [(A, b) for A in range(4) for b in range(4)]
-        if t == 0: setup_moves()
         for j in range(6):
-            for a in range(24 - SSHARE, 24) if j == FFIRST else ():
+            if t == 0 and j < 3: (setup_zeros, setup_columns, setup_moves)[j]()
+            for _ in range(FSHARE[j]):
+                if fq:
+                    A, b = fq.pop(0)
+                    bk = ("PCC", "PD")[rot[0] % 2]
+                    rot[0] += 1
+                    mm(bk, ("QF", 512 * A + 128 * b), ("QX", 0), C)
+                    act(r("FT", 1536 * b + C * A, 1536 * b + C * A + C), r(bk, 0, C), scale=0.5)
+            for a in range(24 - SSHARE, 24) if t and j == FFIRST else ():
                 m = 16 * a + 16
-                x, y = r("TM", C * (a % 2), C * (a % 2) + m), r("C%d" % (a // 4 - 2), a % 4, 4 * m, 4)
-                src, b = r("TS", 0, m), r("NS", a, a + 1)
-                do("S", lambda e: e.activation(ap(x), ap(src), ActivationFunctionType.Relu, bias=ap(b)), [src, b], [x])
-                do("S", lambda e: e.activation(ap(y), ap(x), ActivationFunctionType.Sign), [x], [y])
-            n = "C%d" % (j % 2 if j < 4 else j - 2)
+                x = r("TM", C * (a % 2), C * (a % 2) + m)
+                act(x, r("TS", 0, m), bias=r("NS", a, a + 1), fn=ActivationFunctionType.Relu)
+                act(r("C2", a % 4, 4 * m, 4), x, fn=ActivationFunctionType.Sign)
+            n = "C2" if j == 5 else "C%d" % (j % 2)
             for e in range(4):
                 a = 4 * j + e
                 m = 16 * a + 16
                 col = r("ST", m - 1, m)
-                if a < 24 - SSHARE: ts(r(n, e, 4 * m, 4), r("TS", 0, m), col, OP.is_gt)
+                if t == 0 or a < 24 - SSHARE: ts(r(n, e, 4 * m, 4), r("TS", 0, m), col, OP.is_gt)
                 if m < C: ts(r(n, 4 * m + e, 4 * C, 4), r("TS", m, C), col, OP.is_ge)
             quant("QT", C * j, C * j + C, r(n))
             mm("PB", K("gone"), ("QT", C * j), C, j == 0, j == 5)
@@ -525,37 +531,33 @@ def rank_program(g, core, T, topo):
             if t and j == 1:
                 quant("QIN", 0, 128, r("IN"))
                 inject(True)
-            for _ in range(3):
-                if fq and j < 6:
-                    A, b = fq.pop(0)
-                    bk = ("PCC", "PD")[rot[0] % 2]
-                    rot[0] += 1
-                    mm(bk, ("QF", 512 * A + 128 * b), ("QX", 0), C)
-                    act(r("FT", 1536 * b + C * A, 1536 * b + C * A + C), r(bk, 0, C), scale=0.5)
-        if t == 0: quant_tiles("qsel", "own2")
+        if t == 0:
+            quant_tiles("qsel", "own2")
+            quant("QGA", 192, 320, r("GA", 768, 1280))
         ts(r("GT", 0, C), r("PB", 0, C), float(GW + 1), OP.is_lt)
         quant("QG", 0, 128, r("GT"))
         mm("PA", K("qsel"), ("QG", 0), 128)
         if t == 0:
-            tc(r("LW"), r("IJF"))
+            act(r("LW"), r("IJF"))
+            tt(r("AW", 0, C), r("TS", 0, C), r("NB", 0, C), OP.is_lt, off=r("OFJ", 0, 24))
+            for k, own in ((1, r("NB", C, 2 * C)), (2, r("SB2"))):
+                x = r(("LT", "EQ")[k - 1])
+                tt(x, r("SL", C * k - C, C * k), own, OP.is_lt, off=r("OFJ", 24 * k, 24 * k + 24))
+                act(r("AW", C * k, C * k + C), x, bias=P("g%d" % (2 * k - 2)), scale=P("sg%d" % k), fn=IDENT)
+            tt(r("LE"), r("TS", 0, C), r("NB", 0, C), OP.is_equal, off=r("OFJ", 0, 24))
             tt(r("ML"), r("IJF"), r("LW"), OP.is_lt, off=r("OFJ", 0, 24))
-            for k in range(3):
-                of = r("OFT", 24 * k, 24 * k + 24)
-                le = ("LE", "LT", "EQ")[k]
-                tt(r(le), r("TS"), r("NB", 0, C), OP.is_equal, off=of)
-                if k == 0: tt(r("RF", 0, C), r(le), r("ML"), OP.mult)
-                else: act(r("RF", C * k, C * k + C), r(le), scale=P("g0" if k == 1 else "g2"))
-                tt(r("AW", C * k, C * k + C), r("TS"), r("NB", 0, C), OP.is_lt, off=of)
+            tt(r("RF", 0, C), r("LE"), r("ML"), OP.mult)
+            quant("QRF", 0, 128, r("RF", 0, 512))
             quant("QAW", 0, 320, r("AW"))
-            quant("QRF", 0, 320, r("RF"))
             for k in range(3):
-                for j, n in enumerate(("QAW", "QRF")): mm("PV%d" % k, K("q3"), (n, 96 * k), 128, j == 0, j == 1)
-            for k in range(3):
-                for j, n in enumerate(("QAW", "QRF")): mm("PV3", K("q1_%d" % k), (n, 96 * k), 128, k == 0 and j == 0, k == 2 and j == 1)
+                mm("PV%d" % k, K("q3"), ("QAW", 96 * k), 128, True, k > 0)
+                mm("PV3", K("q1_%d" % k), ("QAW", 96 * k), 128, k == 0, False)
+            mm("PV0", K("q3"), ("QRF", 0), 128, False, True)
+            mm("PV3", K("q1_0"), ("QRF", 0), 128, False, True)
         ts(r("G3"), r("PA", 0, 96), 6.0, OP.mult, -3.0, OP.add)
         ts(r("G9"), r("PA", 0, 96), 9.0, OP.mult, 0.5, OP.add)
 
-        def aux_list():
+        def list1():
             tt(r("SB2"), r("PB", 0, C), r("MD"), OP.mult)
             scan(r("ST2"), r("ND"), r("SB2"))
             ts(r("PLo"), r("ST2", 15, C, 16), -1.0, OP.add)
@@ -595,6 +597,9 @@ def rank_program(g, core, T, topo):
             mm("PA", K("qsel"), ("QRF", 192), 128, False, True)
             act(r("R2"), r("PA", 0, 96), bias=1.0)
 
+        sq = [(A, j) for A in range(4) for j in range(7)]
+        pend = []
+
         def slots(n):
             for _ in range(n):
                 if not sq: return
@@ -607,18 +612,19 @@ def rank_program(g, core, T, topo):
                 A = pend.pop(0)
                 act(r("SL", C * A, C * A + C), r("PCC" if A % 2 == 0 else "PD", 0, C), bias=float(C * A - 1))
 
-        sq = [(A, j) for A in range(4) for j in range(7)]
-        pend = []
         onS = [[scores_at(0)], [scores_at(1)], [gates], [], [], [orders2]]
-        onV = [[aux_list], [list2], [order(0)], [pass_on, order(1)], [orders], []]
+        onV = [[list1], [list2], [order(0)], [pass_on, order(1)], [orders], []]
         if t == 0:
             setup_classes()
-            onS[1].append(setup_hops)
+            for k in range(3): onS[k].append(lambda k=k: setup_hops(k))
+            onS[3].append(setup_tables)
+            for k in range(3):
+                onS[1 + k].append(lambda k=k: setup_ends_s(k))
+                onS[2 + k].append(lambda k=k: setup_ends(k))
             onV[0].append(lambda: quant_tiles("cls0", "cls3"))
             onV[0].append(setup_routes)
-            onV[2].append(lambda: quant_tiles("hop0", "hop2"))
-            onV[2].append(lambda: quant_tiles("hopf0", "gb"))
-            for k in range(3): onV[2 + k].append(lambda k=k: setup_ends(k))
+            onV[3].append(lambda: quant_tiles("hop0", "hop2"))
+            onV[4].append(lambda: quant_tiles("hopf0", "gb"))
             onV[5].append(setup_layer)
         for i in range(SWEEPS):
             tt(r("MA"), r("PV0", 0, 96), r("G3"), OP.max)
@@ -654,49 +660,57 @@ def rank_program(g, core, T, topo):
         tt(r("ub"), r("t1"), r("t2"), OP.add)
         tt(r("PP"), r("ua"), r("ub"), OP.add)
         masked(r("PP"))
-        for h in range(3):
-            last = h == 2
-            gather_w(VHOP)
-            slot_copies()
-            if h == 0:
-                quant("QW", 0, 128, r("W"))
-                mm("PV3", K("hopf0"), ("QW", 0), 128)
-            else:
-                for b in (2 * h - 2, 2 * h - 1):
-                    act(r("FD", C * b, C * b + C), r("FT", 1536 * b, 1536 * b + 1536), off=r("DL"))
-            quant("QGA", 0, 288, r("GA", 0, 1152))
-            for k in range(3): mm(("PA", "PB", "PV2")[k], K("hop%s%d" % ("f" if last else "", k)), ("QGA", 96 * k), 128)
-            slots(SLOTS[SWEEPS + h])
-            if h == 0:
-                to_list(r("PV3", 0, 96), r("DL"))
-                tt(r("SJF"), r("self"), r("JF"), OP.mult)
-            if last:
-                a, o = (0, 0) if t == 0 else (GW * t, 32)
-                for j in range(8):
-                    two = [("PV0", "PV1", "PV3", "PD")[2 * (j % 2) + i] for i in range(2)]
-                    for i in range(2): mm(two[i], ("WP", 256 * j + 128 * i), ("LD", a), 128)
-                    for i in range(2):
-                        b, A = j // 2, 2 * (j % 2) + i
-                        act(r("HT", 1536 * b + C * A, 1536 * b + C * A + GW), r(two[i], o, o + GW), scale=0.015625)
-            for k in range(3): tt(r("t%d" % k), r(("PA", "PB", "PV2")[k], 0, 96), r("pk%d" % k), OP.mult)
-            tt(r("ua"), r("t0"), r("SJF") if last else r("SJ"), OP.add)
-            tt(r("ub"), r("t1"), r("t2"), OP.add)
-            if last:
-                tt(r("PE"), r("ua"), r("ub"), OP.add)
-            else:
-                tt(r("PP"), r("ua"), r("ub"), OP.add)
-                masked(r("PP"))
-        to_list(r("PE"), r("EL"))
-        if t == R - 1: number_parts()
+        gather_w(VHOP)
+        slot_copies()
+        quant("QW", 0, 128, r("W"))
+        mm("PV3", K("hopf0"), ("QW", 0), 128)
+        quant("QGA", 0, 288, r("GA", 0, 1152))
+        for k in range(3): mm("PV%d" % k, K("hop%d" % k), ("QGA", 96 * k), 128)
+        slots(SLOTS[SWEEPS])
+        to_list(r("PV3", 0, 96), r("DL"))
+        for k in range(3): tt(r("t%d" % k), r("PV%d" % k, 0, 96), r("pk%d" % k), OP.mult)
+        tt(r("ua"), r("t0"), r("SJ"), OP.add)
+        tt(r("ub"), r("t1"), r("t2"), OP.add)
+        tt(r("PP"), r("ua"), r("ub"), OP.add)
+        masked(r("PP"))
+        quant("QW", 0, 128, r("W"))
+        mm("PV2", K("ct2"), ("QW", 0), 128)
+        mm("PV0", K("ct0"), ("QW", 0), 128)
+        mm("PA", K("hopf0"), ("QW", 0), 128)
+        mm("PV1", K("ct1"), ("QW", 0), 128)
+        mm("PV3", K("ct3"), ("QW", 0), 128)
+        slot_copies()
+        for A in (2, 3, 0, 1):
+            for s in range(4):
+                o, x = r("WA", C * A + s, C * A + C, 4), r("PV%d" % A, 0, 96)
+                if A < 2: ts(o, x, P("ms%d" % s), OP.mult)
+                else: act(o, x, scale=P("ms%d" % s))
+        to_list(r("PA", 0, 96), r("EL"))
+        act(r("GA", 192, C), r("WA"), off=r("EL", 12, 24))
+        tc(r("GA", 0, 192), r("WA"), off=r("EL", 0, 12))
+        for b in range(4):
+            act(r("FD", C * b, C * b + C), r("FT", 1536 * b, 1536 * b + 1536), off=r("DL"))
+        quant("QG", 0, 128, r("GA", 0, 512))
+        mm("PB", K("hopf0"), ("QG", 0), 128)
+        a, o = (0, 0) if t == 0 else (GW * t, 32)
+        for j in range(8):
+            two = [("PV0", "PV1", "PV2", "PV3")[2 * (j % 2) + i] for i in range(2)]
+            for i in range(2): mm(two[i], ("WP", 256 * j + 128 * i), ("LD", a), 128)
+            for i in range(2):
+                b, A = j // 2, 2 * (j % 2) + i
+                act(r("HT", 1536 * b + C * A, 1536 * b + C * A + GW), r(two[i], o, o + GW), scale=0.015625)
+        to_list(r("PB", 0, 96), r("EL"))
+        if t == R - 1:
+            tc(r("PE"), r("PB", 0, 96))
+            number_parts()
         tt(r("SB2"), r("SL"), r("MD"), OP.mult, off=r("EL"))
         scan(r("ST2"), r("ND"), r("SB2"))
         tc(r("HL"), r("ST2", 15, C, 16))
         for b in range(4):
             tt(r("Z", C * b, C * b + C), r("FT", 1536 * b, 1536 * b + 1536), r("FD", C * b, C * b + C), OP.add, off=r("EL"))
-        xn = "X1"
         for b in range(4):
-            tt(r(xn, b, 4 * C, 4), r("HT", 1536 * b, 1536 * b + 1536), r("Z", C * b, C * b + C), OP.add, off=r("HL"))
-        quant("QX", 0, C, r(xn))
+            tt(r("X0", b, 4 * C, 4), r("HT", 1536 * b, 1536 * b + 1536), r("Z", C * b, C * b + C), OP.add, off=r("HL"))
+        quant("QX", 0, C, r("X0"))
         if t == 0: quant("QV", 0, 128, r("VV"))
     mm("PA", ("QV", 0), ("QX", 0), C)
     act(r("TS", 2 * C, 3 * C), r("PA", 0, C))

import math
from concourse.bass import DstId, RemoteDMATransfer
from concourse.mybir import dt, AluOpType, AxisListType, ActivationFunctionType

OP = AluOpType
COPY, IDENT = ActivationFunctionType.Copy, ActivationFunctionType.Identity
C, GW, R, SWEEPS = 384, 96, 3, 6
JUMP = [0, 1, 4]

TILES = ["gone", "qsel", "qneg", "q3", "q1_0", "q1_1", "q1_2", "st0", "st1", "st2", "sto", "came0", "came1", "came2",
         "own0", "own1", "own2", "hop0", "hop1", "hop2", "cls0", "cls1", "cls2", "cls3", "hopf0", "ct0", "ct1", "ct2", "ct3", "ge", "gm", "gb"]
TI = {n: i for i, n in enumerate(TILES)}
NT = len(TILES)
VSWEEP = [0, 448, 352, 320, 224, 512]
VHOP = 512
SLOTS = [4, 4, 4, 4, 4, 4, 4]
FSHARE = [6, 4, 3, 3, 0, 0]
FFIRST = 2
SSHARE = 3
ENGINES = 8

F32, BF, I32, U16, X4, U8 = "float32", "bfloat16", "int32", "uint16", "float8_e4m3fn_x4", "uint8"
SCRATCH = {}
WIDE = {"KF": "JM MD ND IJF CMr RM J0 J1 J2 D0 D1 D2", "KI": "PC UL WL", "XI": "EI EP",
        "XF": "SB1 ST SB2 ST2 SB3 ST3 t0 t1 t2 ua ub PE la lb lc qa qb qd qm ea eb ec ba bb",
        "XB": "G3 G9 MA MB MC TU R0 R1 R2 va0 va1 va2 mx0 mx1 mx2 pk0 pk1 pk2 self SJ PP OC0 OC1 OC2 JC EQ LT LE ML"}
HOME = {n: w for w in WIDE for n in WIDE[w].split()}
PLACE, LEN = {}, {}


def sb(name, n, d):
    w = HOME.get(name, name)
    a = SCRATCH[w][1][1] if w in SCRATCH else 0
    PLACE[name], LEN[name] = (w, a), n
    SCRATCH[w] = ("sbuf", [128, a + (n if w == name else (n + 15) // 16 * 16)], d)


def mx(name, n):
    sb(name + "c", n, X4)
    sb(name + "s", n, U8)


for _n, _w, _d in [
        ("X0", 1536, BF), ("U", 512, BF), ("VV", 512, BF),
        ("LKT", 72, I32), ("LKS", 72, I32), ("OFT", 72, U16), ("OFJ", 72, U16), ("OFS", 72, U16),
        ("UL", 24, I32), ("ULo", 24, U16), ("WL", 128, I32), ("WLo", 128, U16),
        ("PC", 16, I32), ("PF", 48, F32), ("WT", 1024, BF), ("CB", 512 * NT, BF), ("FB", 4 * 516, BF),
        ("GC", 96, BF), ("GCt", 96, BF), ("GD", 128, BF), ("GDt", 128, BF), ("GH", 96, BF), ("KM", 32, BF), ("GOt", 512, BF),
        ("JM", C, F32), ("MD", C, F32), ("ND", C, F32), ("MX", C, F32), ("NX", C, F32), ("NS", 24, F32), ("TM", 2 * C, BF), ("IJF", C, F32),
        ("CMr", 96, F32), ("RM", 96, F32), ("J0", 96, F32), ("J1", 96, F32), ("J2", 96, F32), ("qm", C, F32),
        ("TS", 3 * C, F32), ("SB1", C, F32), ("ST", C, F32), ("EQ", C, BF), ("ET", 4 * C, BF),
        ("GT", 512, BF), ("G3", 96, BF), ("G9", 96, BF), ("PLo", 24, U16), ("LW", C, F32), ("SB2", C, F32),
        ("ST2", C, F32), ("SB3", GW, F32), ("ST3", GW, F32), ("ELo", 6, U16),
        ("FT", 16 * C, BF), ("HT", 16 * C, BF), ("SL", 4 * C, F32), ("FD", 4 * C, BF), ("Z", 4 * C, BF), ("WA", 4 * C, BF),
        ("LT", C, BF), ("LE", C, BF), ("ML", C, BF), ("AW", 1280, BF), ("RF", 1280, BF), ("NB", 2 * C, F32),
        ("MA", 96, BF), ("MB", 96, BF), ("MC", 96, BF), ("IN", 512, BF), ("TU", 96, BF), ("W", 512, BF), ("GA", 1280, BF),
        ("R0", 96, BF), ("R1", 96, BF), ("R2", 96, BF), ("va0", 96, BF), ("va1", 96, BF), ("va2", 96, BF),
        ("mx0", 96, BF), ("mx1", 96, BF), ("mx2", 96, BF), ("pk0", 96, BF), ("pk1", 96, BF), ("pk2", 96, BF),
        ("self", 96, BF), ("SJ", 96, BF), ("t0", 96, F32), ("t1", 96, F32), ("t2", 96, F32),
        ("ua", 96, F32), ("ub", 96, F32), ("PP", 96, BF), ("PE", 96, F32),
        ("la", 96, F32), ("lb", 48, F32), ("lc", 24, F32), ("DL", 24, U16), ("EL", 24, U16), ("HL", 24, U16),
        ("D0", C, F32), ("D1", C, F32), ("D2", C, F32), ("CTF", C, F32),
        ("qa", C, F32), ("qb", 192, F32), ("qd", 96, F32), ("OC0", 96, BF), ("OC1", 96, BF), ("OC2", 96, BF), ("JC", 96, BF),
        ("ea", 96, F32), ("eb", 96, F32), ("ec", 96, F32), ("EI", 96, I32), ("EP", 288, I32), ("ba", 96, F32), ("bb", 96, F32),
        ("C0", 4 * C, BF), ("C1", 4 * C, BF), ("C2", 4 * C, BF), ("E0", 512, BF), ("E1", 512, BF), ("E2", 512, BF)]:
    sb(_n, _w, _d)
for _n, _w in [("QX", C), ("QU", 128), ("QUP", C), ("QV", 128), ("WC", 512), ("WP", 2048), ("QK", 128 * NT), ("QF", 2048),
               ("QT", 7 * C), ("QG", 128), ("QAW", 320), ("QRF", 320), ("QIN", 128), ("QGA", 320), ("QW", 128),
               ("QE", 3 * 128), ("LD", 320), ("QND", C)]:
    mx(_n, _w)
PS = ["PV0", "PV1", "PV2", "PV3", "PA", "PB", "PCC", "PD"]
for _n in PS:
    SCRATCH[_n] = ("psum", [128, 512], F32)
    PLACE[_n], LEN[_n] = (_n, 0), 512
SEMAPHORES = ["sv", "ss", "st", "sg", "lcl", "arr0", "arr1", "arr2"] + ["d%d" % i for i in range(10)]


def rank_program(g, core, T, topo):
    rank = T.rank_of(core)
    if rank is None:
        return
    nxt = T.cores[(rank + 1) % len(T.cores)]
    Q = {"V": g.vector, "S": g.scalar, "T": g.tensor, "G": g, "Y": g.sync}
    SEM = {"V": "sv", "S": "ss", "T": "st", "G": "sg"}
    cnt = {s: 0 for s in SEMAPHORES}
    known = {q: {} for q in Q}
    clk, wrs, rds, bank = {}, {}, {}, {}

    def overlap(a, b):
        if a[1] <= b[0] or b[1] <= a[0]: return False
        d = math.gcd(a[2], b[2])
        return not (d > 1 and (a[0] - b[0]) % d)

    def await_(q, deps):
        best = {}
        for s, c in deps:
            best[s] = max(best.get(s, 0), c)
        for s, c in sorted(best.items(), key=lambda t: -t[1]):
            if known[q].get(s, 0) >= c: continue
            Q[q].wait_ge(T.sem[s], c)
            known[q][s] = c
            for s2, c2 in clk[(s, c)].items():
                if known[q].get(s2, 0) < c2: known[q][s2] = c2

    def deps_of(q, rd, wr):
        deps = []
        for n, lo, hi, st in rd:
            if n in PS: continue
            for e in wrs.get(n, []):
                if overlap(e[0], (lo, hi, st)): deps.append(e[1])
        for n, lo, hi, st in wr:
            if n in PS: continue
            for e in wrs.get(n, []):
                if overlap(e[0], (lo, hi, st)): deps.append(e[1])
            for e in rds.get(n, []):
                if overlap(e[0], (lo, hi, st)): deps.append(e[1])
        for n in set(x[0] for x in list(rd) + list(wr) if x[0] in PS):
            for q2, m in bank.get(n, {}).items():
                if q2 != q: deps.append(m)
        return deps

    def record(q, m, rd, wr):
        for n, lo, hi, st in wr:
            if n in PS: continue
            for tab in (wrs, rds):
                tab[n] = [e for e in tab.get(n, []) if not (e[0][0] >= lo and e[0][1] <= hi and (st == 1 or (e[0][2] == st and e[0][0] == lo)))]
            wrs[n].append(((lo, hi, st), m, q))
        for n, lo, hi, st in rd:
            if n in PS: continue
            rds[n] = [e for e in rds.get(n, []) if not (e[2] == q and q != "D" and e[0] == (lo, hi, st))] + [((lo, hi, st), m, q)]
        for n in set(x[0] for x in list(rd) + list(wr) if x[0] in PS):
            b = bank.get(n, {})
            b = {q2: m2 for q2, m2 in b.items() if q2 == q or known[q].get(m2[0], 0) < m2[1]}
            b[q] = m
            bank[n] = b

    def do(q, fn, rd, wr):
        await_(q, deps_of(q, rd, wr))
        s = SEM[q]
        cnt[s] += 1
        m = (s, cnt[s])
        fn(Q[q]).then_inc(T.sem[s], 1)
        c = dict(known[q])
        c[s] = cnt[s]
        clk[m] = c
        record(q, m, rd, wr)

    def dma(q, s, pairs, rd=(), wr=()):
        await_(q, deps_of("D", rd, wr))
        for o, i in pairs:
            Q[q].dma_start(o, i).then_inc(T.sem[s], 16)
            cnt[s] += 16
        m = (s, cnt[s])
        c = dict(known[q])
        c[s] = cnt[s]
        clk[m] = c
        record("D", m, rd, wr)

    def r(n, lo=0, hi=None, st=1):
        w, a = PLACE[n]
        return (w, a + lo, a + (LEN[n] if hi is None else hi), st)

    def ap(x):
        n, lo, hi, st = x
        return T[n][:, lo:hi] if st == 1 else T[n][:, lo:hi:st]

    isr = lambda x: isinstance(x, tuple)
    val = lambda x: ap(x) if isr(x) else x

    def ts(o, i, s1, op0, s2=None, op1=None):
        rd = [i] + [s for s in (s1, s2) if isr(s)]
        if op1 is None: do("V", lambda e: e.tensor_scalar(ap(o), ap(i), val(s1), None, op0), rd, [o])
        else: do("V", lambda e: e.tensor_scalar(ap(o), ap(i), val(s1), val(s2), op0, op1), rd, [o])

    def tt(o, a, b, op, off=None):
        if off is None: do("V", lambda e: e.tensor_tensor(ap(o), ap(a), ap(b), op), [a, b], [o])
        else: do("V", lambda e: e.tensor_tensor(ap(o), ap(a).indirect(ap(off)), ap(b), op), [a, b, off], [o])

    def tc(o, a, off=None):
        if off is None: do("V", lambda e: e.tensor_copy(ap(o), ap(a)), [a], [o])
        else: do("V", lambda e: e.tensor_copy(ap(o), ap(a).indirect(ap(off))), [a, off], [o])

    def act(o, a, bias=0.0, scale=1.0, off=None, fn=COPY):
        rd = [a] + [x for x in (scale, bias, off) if isr(x)]
        if off is None: do("S", lambda e: e.activation(ap(o), ap(a), fn, bias=val(bias), scale=val(scale)), rd, [o])
        else: do("S", lambda e: e.activation(ap(o), ap(a).indirect(ap(off)), fn, bias=val(bias), scale=val(scale)), rd, [o])

    def scan(o, a, b, op0=OP.mult, op1=OP.add):
        do("V", lambda e: e.tensor_tensor_scan(ap(o), ap(a), ap(b), 0.0, op0, op1), [a, b], [o])

    def fill(o, c):
        do("V", lambda e: e.memset(ap(o), c), [], [o])

    def quant(n, a, b, src):
        q, s = r(n + "c", a, b), r(n + "s", a, b)
        do("V", lambda e: e.quantize_mx(ap(q), ap(s), ap(src)), [src], [q, s])

    def pick(n, src, k, off):
        m, w = 16 * (off[2] - off[1]), LEN[src + "c"]
        do("V", lambda e: e.tensor_copy(T[n + "c"][:, 0:m].bitcast(dt.uint32), T[src + "c"][:, 0:w].bitcast(dt.uint32).indirect(ap(off))), [r(src + "c"), off], [r(n + "c")])
        do("S", lambda e: e.activation(T[n + "s"][:, 0:m], T[src + "s"][:, 0:w].indirect(ap(off)), COPY), [r(src + "s"), off], [r(n + "s")])

    def mm(bk, st, mv, n, start=True, stop=True):
        l, ls = r(st[0] + "c", st[1], st[1] + 128), r(st[0] + "s", st[1], st[1] + 128)
        m, ms = r(mv[0] + "c", mv[1], mv[1] + n), r(mv[0] + "s", mv[1], mv[1] + n)
        o = r(bk, 0, n)
        do("T", lambda e: e.matmul_mx(ap(o), ap(l), ap(ls), ap(m), ap(ms), start, stop), [l, ls, m, ms], [o])

    def iota(o, pat, base, cm):
        fl = SCRATCH[o[0]][2] != I32
        if fl: do("G", lambda e: e.iota(ap(o), pat, base, cm, allow_small_or_imprecise_dtypes=True), [], [o])
        else: do("G", lambda e: e.iota(ap(o), pat, base, cm), [], [o])

    def sel(o, i, pat, op, fl, base, cm):
        do("G", lambda e: e.affine_select(ap(o), ap(i), pat, op, fl, base, cm), [i], [o])

    K = lambda n: ("QK", 128 * TI[n])
    tile0 = lambda n: 512 * TI[n]
    tile = lambda n, a=0, st=1: r("CB", tile0(n) + a, tile0(n) + 512, st)

    dma("Y", "d0", [(T.X0[:], T.x[:])], wr=[r("X0")])
    dma("S", "d1", [(T.U[:], T.u[:])], wr=[r("U")])
    dma("Y", "d2", [(T.LKT[:], T.lk[:])], wr=[r("LKT")])
    pr = [(T.LKS[:, 0:24], T.lk[:, 0:24])]
    for h in range(8):
        a = h ^ JUMP[1]
        pr.append((T.LKS[16 * h:16 * h + 16, 24:48], T.lk[16 * a:16 * a + 16, 24:48]))
    for h in range(0, 8, 4):
        a = h ^ JUMP[2]
        pr.append((T.LKS[16 * h:16 * h + 64, 48:72], T.lk[16 * a:16 * a + 64, 48:72]))
    dma("Y", "d3", pr, wr=[r("LKS")])
    dma("Y", "d4", [(T.WCc[:].bitcast(dt.uint8), T.wc[:]), (T.WCs[:], T.ws[:])], wr=[r("WCc"), r("WCs")])
    dma("Y", "d5", [(T.VV[:], T.v[:])], wr=[r("VV")])

    GRP = {0: ([[16, 8]], 0), 1: ([[32, 4], [-16, 2]], 16), 4: ([[-64, 2], [16, 4]], 64)}
    CLS = lambda A: 16 * (A & 1) + 64 * (A >> 1)
    neg = lambda pat: [[-a, b] for a, b in pat]
    for k in range(3):
        iota(r("UL", 8 * k, 8 * k + 8), GRP[JUMP[k]][0], GRP[JUMP[k]][1], 0)
    iota(r("PC", 0, 1), [[0, 1]], 0, 1)
    iota(r("JM"), [[0, 24], [1, 16]], 0, 0)
    fill(r("WT", 0, 512), 1.0)
    for j, w in enumerate([-6.0, -2.0, 3.0, -1.0]):
        fill(r("WT", 512 + 128 * j, 640 + 128 * j), w)
    WCOL = {1.0: 0, -6.0: 512, -2.0: 640, 3.0: 768, -1.0: 896}
    tc(r("ULo"), r("UL"))
    for a in (0, 1024): act(r("FB", a, a + 1024), r("WT", 0, 1024), scale=0.0)
    act(r("FB", 2048), r("WT", 0, 16), scale=0.0)
    PFC = {}

    def pcol(name):
        PFC[name] = len(PFC)
        return r("PF", PFC[name], PFC[name] + 1)

    P = lambda name: r("PF", PFC[name], PFC[name] + 1)

    def scol(name, a, scale=1.0, bias=0.0):
        act(pcol(name), P(a), bias=bias, scale=scale, fn=IDENT if isr(bias) else COPY)

    p = r("PC", 0, 1)
    for j, (n, sh, an) in enumerate([("i", 0, 15), ("s", 0, 3), ("kk", 2, 3), ("g0", 4, 1), ("g1", 5, 1), ("g2", 6, 1)]):
        o = r("PC", j + 1, j + 2)
        ts(o, p, sh, OP.arith_shift_right, an, OP.bitwise_and)
        tc(pcol(n), o)
    ts(r("MD"), r("JM"), P("i"), OP.is_equal)
    act(r("MX"), r("MD"), scale=2e29, bias=-1e29)
    act(r("ND"), r("MD"), scale=-1.0, bias=1.0)
    act(r("NX"), r("MD"), scale=-2e29)
    for A in range(4):
        for h in range(2):
            a = 516 * A + 3 + 256 * h
            sel(r("FB", a, a + 253, 4), r("WT", 0, 64), [[-32, 2], [0, 2], [-1, 16]], OP.is_equal, 0.0, -CLS(A), 1)
    for k in range(3):
        gp, gb = GRP[JUMP[k]]
        sel(r("GCt", 32 * k, 32 * k + 32), r("WT", 0, 32), neg(gp) + [[0, 4]], OP.is_ge, 0.0, -gb, 1)
        sel(r("GC", 32 * k, 32 * k + 32), r("GCt", 32 * k, 32 * k + 32), gp + [[0, 4]], OP.is_ge, 0.0, gb + 15, -1)
    sel(r("NX"), r("NX"), [[0, 24], [1, 16]], OP.not_equal, -2e29, 0, 0)
    sel(r("GOt"), r("WT", 0, 512), [[-16, 8], [0, 64]], OP.is_ge, 0.0, 0, 1)
    sel(tile("gone"), r("GOt"), [[16, 8], [0, 64]], OP.is_ge, 0.0, 15, -1)

    def zeros(a, b):
        while a < b:
            n = min(1024, b - a)
            act(r("CB", a, a + n), r("WT", 0, n), scale=0.0)
            a += n

    z0, zc = tile0("qsel"), tile0("came0")
    quant("QU", 0, 128, r("U"))
    zeros(zc, zc + 2048)
    pick("QUP", "QU", 3, r("ULo"))
    quant("QX", 0, C, r("X0"))

    def scores():
        mm("PA", ("QUP", 0), ("QX", 0), C)
        mm("PB", ("QUP", 0), ("QX", 0), C)
        mm("PCC", ("QUP", 128), ("QX", 0), C)
        mm("PD", ("QUP", 256), ("QX", 0), C)
        act(r("TS", 0, C), r("PB", 0, C))
        act(r("TS", C, 2 * C), r("PCC", 0, C))
        act(r("TS", 2 * C, 3 * C), r("PD", 0, C))

    scores()
    act(r("NB", 0, C), r("PB", 0, C))
    for k, n in ((1, "g0"), (2, "g2")): scol("sg%d" % k, n, -2.0, 1.0)
    act(r("NB", C, 2 * C), r("PB", 0, C), scale=P("sg1"))
    act(r("SB2"), r("PB", 0, C), scale=P("sg2"))
    act(r("SL", 0, C), r("PCC", 0, C), scale=P("sg1"))
    act(r("SL", C, 2 * C), r("PD", 0, C), scale=P("sg2"))
    act(r("RF", C, 512), r("WT", 0, 512 - C), scale=0.0)

    def setup_first():
        quant("QK", 0, 128, tile("gone"))
        for A in range(4):
            for b in range(4):
                quant("QF", 512 * A + 128 * b, 512 * A + 128 * b + 128, r("FB", 516 * A + 3 - b, 516 * A + 515 - b))

    fill(r("CB", z0, zc), 0.0)
    for n, a in (("GT", C), ("W", C), ("GA", 1152), ("AW", 1152), ("RF", 1152)):
        fill(r(n, a), 0.0)
    for t in range(R):
        fill(r("E%d" % t, 4 * GW, 512), 0.0)

    def setup_zeros():
        zeros(zc + 2048, tile0("hop0"))
        for a in (0, 768): act(r("ET", a, a + 768), r("WT", 0, 768), scale=0.0)
        act(r("IN"), r("WT", 0, 512), scale=0.0)
        act(r("GA", 640, 1152), r("WT", 0, 512), scale=0.0)

    iota(r("IJF"), [[1, C]], 0, 0)
    for n, w in (("qsel", 1.0), ("qneg", -1.0), ("q3", 3.0)):
        for s in range(4):
            sel(tile(n, 5 * s, 16), r("WT", WCOL[w], WCOL[w] + 32), [[-16, 8], [-4, 4]], OP.is_equal, 0.0, -s, 1)
    for k in range(3):
        for s in range(4):
            sel(tile("q1_%d" % k, 16 * k + 5 * s, 64), r("WT", 0, 8), [[-16, 8]], OP.is_equal, 0.0, -4 * k - s, 1)
    for k in range(3):
        for e in (0, 1 + k): sel(tile("st%d" % k, e, 4), r("WT", WCOL[3.0], WCOL[3.0] + 128), [[-1, 128]], OP.is_equal, 0.0, 0, 1)
    sel(tile("sto", 0, 4), r("WT", 0, 128), [[-1, 128]], OP.is_equal, 0.0, 0, 1)
    for k in range(3):
        for s in range(4): sel(tile("sto", 16 * k + 4 * s + 1 + k, 64), r("WT", 0, 8), [[-16, 8]], OP.is_equal, 0.0, -4 * k - s, 1)
    for A in range(4):
        a = 32 * A
        sel(r("GDt", a, a + 32), r("WT", 0, 32), [[0, 2], [-32, 2], [0, 8]], OP.is_ge, 0.0, -CLS(A), 1)
        sel(r("GD", a, a + 32), r("GDt", a, a + 32), [[0, 2], [32, 2], [0, 8]], OP.is_ge, 0.0, CLS(A) + 15, -1)
    iota(r("CMr"), [[0, 24], [1, 4]], 0, 0)
    iota(r("D0"), [[0, 48], [1, 8]], 0, 0)
    iota(r("D1"), [[0, 6], [8, 8], [0, 8]], 0, 0)
    iota(r("D2"), [[64, 6], [0, 64]], 0, 0)
    iota(r("J0"), [[0, 48], [4, 2]], 0, 0)
    iota(r("J1"), [[0, 6], [8, 8], [0, 2]], 0, 0)
    iota(r("J2"), [[64, 6], [0, 16]], 0, 0)
    iota(r("CB", tile0("hop0"), tile0("cls0")), [[0, 1536]], 0, 0)
    iota(r("CB", tile0("hopf0"), tile0("gb") + 512), [[0, 512 * (TI["gb"] + 1 - TI["hopf0"])]], 0, 0)
    for b in range(4):
        for A in range(4):
            a = 32 * b + 8 * A
            iota(r("WL", a, a + 8), [[0, 2], [32, 2], [0, 2]], 128 * b + CLS(A), 0)
    iota(r("HT"), [[0, 16 * C]], 0, 0)

    def quant_tiles(a, b):
        a, b = TI[a], TI[b] + 1
        while a < b:
            n = min(4, b - a)
            quant("QK", 128 * a, 128 * (a + n), r("CB", 512 * a, 512 * (a + n)))
            a += n

    tc(r("OFT", 0, 24), r("LKT", 0, 24))
    for k in (1, 2): ts(r("OFT", 24 * k, 24 * k + 24), r("LKT", 24 * k, 24 * k + 24), float(C * k), OP.add)
    tc(r("OFJ"), r("LKT"))
    tc(r("OFS"), r("LKS"))
    for s in range(4): ts(pcol("ms%d" % s), P("s"), float(s), OP.is_equal)
    for k in range(4): ts(pcol("mr%d" % k), P("kk"), float(k), OP.is_equal)

    def setup_columns():
        for k in range(3):
            scol("mc%d" % k, "mr%d" % k, -6.0)
            scol("mw%d" % k, "mr%d" % k, -2.0)
        scol("A2", "g2", 2.0, P("g0"))
        scol("A384", "A2", 384.0)
        scol("a3s", "A384", P("mr3"))
        for k, n, f in ((1, "g0", 384.0), (2, "g2", 768.0)):
            scol("x%d" % k, n, -2.0 * f, f)
            scol("y%d" % k, "x%d" % k, 1.0, P("A384"))
            scol("z%d" % k, "y%d" % k, P("mr3"))
        scol("h768", "g1", 768.0)
        scol("b1", "mr1", 2.0, P("mr0"))
        scol("bit", "mr2", 4.0, P("b1"))
        scol("bit8", "bit", 8.0)
        for s in range(4): scol("mo%d" % s, "ms%d" % s, P("mr0"))

    def setup_moves():
        for k in range(3):
            for s in range(4):
                act(tile("came%d" % k, 5 * s, 16), r("GC", 32 * k, 32 * k + 32), scale=P("mc%d" % k))
                act(tile("own%d" % k, 16 * k + 5 * s, 64), r("GC", 32 * k + k, 32 * k + 32, 4), scale=P("mw%d" % k))

    def setup_classes():
        for A in range(4):
            for h in range(4):
                o, src = tile0("cls%d" % A) + 128 * h, tile0("gone") + 64 * ((A & 1) + 2 * (h & 1) + 4 * (A >> 1))
                for g0 in range(2): act(r("CB", o + 64 * g0, o + 64 * g0 + 64), r("CB", src, src + 64))

    def setup_hops(k):
        if k == 0: ts(r("KM"), r("CMr", 0, 32), P("kk"), OP.is_equal)
        h = r("GH", 32 * k, 32 * k + 32)
        tt(h, r("GC", 32 * k, 32 * k + 32), r("KM"), OP.mult)
        for s in range(4): act(tile("hop%d" % k, 5 * s, 16), h)

    def setup_tables():
        for s in range(4): act(tile("hopf0", 5 * s, 16), r("GC", 0, 32))
        for A in range(4):
            d = r("GD", 32 * A, 32 * A + 32)
            tt(d, d, r("KM"), OP.mult)
            for s in range(4): act(tile("ct%d" % A, 5 * s, 16), d)
        for e, n in ((0, "ge"), (1, "ge"), (2, "gm"), (3, "gb")):
            act(tile(n, e, 4), tile("gone", e, 4))

    def setup_routes():
        ts(r("RM"), r("CMr"), P("kk"), OP.is_equal)
        for d in range(3): act(r("D%d" % d), r("D%d" % d), scale=P("mr%d" % d))
        tt(r("qa"), r("D0"), r("D1"), OP.add)
        tt(r("CTF"), r("qa"), r("D2"), OP.add)
        ts(r("t0"), r("J0"), P("s"), OP.add, P("mr0"), OP.mult)
        ts(r("t1"), r("J1"), P("mr1"), OP.mult, P("a3s"), OP.add)
        ts(r("t2"), r("J2"), P("mr2"), OP.mult)
        tt(r("ua"), r("t0"), r("t1"), OP.add)
        tt(r("JC"), r("ua"), r("t2"), OP.add)

    def setup_ends_s(k):
        act(r("qa"), r("CTF"), off=r("OFJ", 24 * k, 24 * k + 24))
        for s in range(4): act(r("qm", 96 * s, 96 * s + 96), r("qa", s, C, 4), scale=P("ms%d" % s))

    def setup_ends(k):
        tt(r("qb"), r("qm", 0, 192), r("qm", 192, C), OP.add)
        tt(r("qd"), r("qb", 0, 96), r("qb", 96, 192), OP.add)
        ts(r("OC%d" % k), r("qd"), P("a3s") if k == 0 else P("z%d" % k), OP.add)

    def setup_layer():
        ts(r("WLo"), r("WL"), P("i"), OP.add)
        pick("WP", "WC", 16, r("WLo"))

    def masked(src):
        for s in range(4):
            o = r("W", s, C, 4)
            if s < 2: ts(o, src, P("ms%d" % s), OP.mult)
            else: act(o, src, scale=P("ms%d" % s))

    def gather_w(n):
        v = n // 16
        win = r("W", 0, C)
        act(r("GA", n, 1152), win, off=r("OFS", v, 72))
        if n: tc(r("GA", 0, n), win, off=r("OFS", 0, v))

    def to_list(src, o):
        tt(r("la"), src, r("RM"), OP.mult)
        tt(r("lb"), r("la", 0, 96, 2), r("la", 1, 96, 2), OP.add)
        tt(r("lc"), r("lb", 0, 48, 2), r("lb", 1, 48, 2), OP.add)
        tc(o, r("lc"))

    def send(t):
        m = topo.engines(core, nxt)[:ENGINES]
        mask = sum(1 << e for e in m)
        rid, pid, _ = topo.addr(nxt)
        n = 128 if t == 0 else GW
        a = 0 if t == 0 else 32 + GW * t
        c, s = r("QEc", 128 * t, 128 * t + n), r("QEs", 128 * t, 128 * t + n)
        await_("G", deps_of("D", [c, s], []))
        sem = T.sem["arr%d" % t]
        g.remote_dma(T.LDc[:, a:a + n].bitcast(dt.uint8), T.QEc[:, 128 * t:128 * t + n].bitcast(dt.uint8), sem, T.sem.lcl, pid, rid, mask)
        g.remote_dma(T.LDs[:, a:a + n], T.QEs[:, 128 * t:128 * t + n], sem, T.sem.lcl, pid, rid, mask)
        cnt["lcl"] += 2 * len(m)
        pe = len(topo.engines(T.cores[(rank - 1) % len(T.cores)], core)[:ENGINES])
        cnt["arr%d" % t] = 2 * pe
        clk[("arr%d" % t, 2 * pe)] = {}
        record("D", ("arr%d" % t, 2 * pe), [], [r("LDc", a, a + n), r("LDs", a, a + n)])

    def state():
        for k in range(3): act(r("IN", 1 + k, 4 * 96, 4), r("PV%d" % k, 0, 96), scale=1.0 / 3.0)

    def inject(stop):
        for k in range(3): mm("PV%d" % k, K("st%d" % k), ("QIN", 0), 128, True, stop)
        mm("PV3", K("sto"), ("QIN", 0), 128, True, stop)

    def number_parts():
        ts(r("ea"), r("PE"), 768.0, OP.is_ge, 768.0, OP.mult)
        tt(r("eb"), r("PE"), r("ea"), OP.add)
        ts(r("ec"), r("eb"), P("h768"), OP.add)
        tc(r("EI"), r("ec"))
        for e, m in enumerate((15, 240, 3840)): ts(r("EP", 96 * e, 96 * e + 96), r("EI"), m, OP.bitwise_and)
        tc(r("qa", 0, 288), r("EP"))
        tt(r("ea"), r("ba"), r("bb"), OP.add)
        for s in range(4):
            for e in range(3): act(r("ET", 4 * s + e, 4 * C, 16), r("qa", 96 * e, 96 * e + 96), scale=P("mo%d" % s))
            act(r("ET", 4 * s + 3, 4 * C, 16), r("ea"), scale=P("ms%d" % s))

    rot = [0]
    for t in range(R):
        if t: scores()
        tt(r("SB1"), r("PA", 0, C), r("MX"), OP.min)
        scan(r("ST"), r("NX"), r("SB1"), OP.add, OP.max)
        ts(r("NS"), r("ST", 15, C, 16), -1.0, OP.mult)
        if t == 0: setup_first()
        fq = [(A, b) for A in range(4) for b in range(4)]
        for j in range(6):
            if t == 0 and j < 3: (setup_zeros, setup_columns, setup_moves)[j]()
            for _ in range(FSHARE[j]):
                if fq:
                    A, b = fq.pop(0)
                    bk = ("PCC", "PD")[rot[0] % 2]
                    rot[0] += 1
                    mm(bk, ("QF", 512 * A + 128 * b), ("QX", 0), C)
                    act(r("FT", 1536 * b + C * A, 1536 * b + C * A + C), r(bk, 0, C), scale=0.5)
            for a in range(24 - SSHARE, 24) if t and j == FFIRST else ():
                m = 16 * a + 16
                x = r("TM", C * (a % 2), C * (a % 2) + m)
                act(x, r("TS", 0, m), bias=r("NS", a, a + 1), fn=ActivationFunctionType.Relu)
                act(r("C2", a % 4, 4 * m, 4), x, fn=ActivationFunctionType.Sign)
            n = "C2" if j == 5 else "C%d" % (j % 2)
            for e in range(4):
                a = 4 * j + e
                m = 16 * a + 16
                col = r("ST", m - 1, m)
                if t == 0 or a < 24 - SSHARE: ts(r(n, e, 4 * m, 4), r("TS", 0, m), col, OP.is_gt)
                if m < C: ts(r(n, 4 * m + e, 4 * C, 4), r("TS", m, C), col, OP.is_ge)
            quant("QT", C * j, C * j + C, r(n))
            mm("PB", K("gone"), ("QT", C * j), C, j == 0, j == 5)
            if j == 4:
                tt(r("ET", 0, 4 * C, 4), r("PA", 0, C), r("ST"), OP.is_equal)
                quant("QT", 6 * C, 7 * C, r("ET"))
                mm("PB", K("gone"), ("QT", 6 * C), C, False, False)
            if t and j == 1:
                quant("QIN", 0, 128, r("IN"))
                inject(True)
        if t == 0:
            quant_tiles("qsel", "own2")
            quant("QGA", 192, 320, r("GA", 768, 1280))
        ts(r("GT", 0, C), r("PB", 0, C), float(GW + 1), OP.is_lt)
        quant("QG", 0, 128, r("GT"))
        mm("PA", K("qsel"), ("QG", 0), 128)
        if t == 0:
            act(r("LW"), r("IJF"))
            tt(r("AW", 0, C), r("TS", 0, C), r("NB", 0, C), OP.is_lt, off=r("OFJ", 0, 24))
            for k, own in ((1, r("NB", C, 2 * C)), (2, r("SB2"))):
                x = r(("LT", "EQ")[k - 1])
                tt(x, r("SL", C * k - C, C * k), own, OP.is_lt, off=r("OFJ", 24 * k, 24 * k + 24))
                act(r("AW", C * k, C * k + C), x, bias=P("g%d" % (2 * k - 2)), scale=P("sg%d" % k), fn=IDENT)
            tt(r("LE"), r("TS", 0, C), r("NB", 0, C), OP.is_equal, off=r("OFJ", 0, 24))
            tt(r("ML"), r("IJF"), r("LW"), OP.is_lt, off=r("OFJ", 0, 24))
            tt(r("RF", 0, C), r("LE"), r("ML"), OP.mult)
            quant("QRF", 0, 128, r("RF", 0, 512))
            quant("QAW", 0, 320, r("AW"))
            for k in range(3):
                mm("PV%d" % k, K("q3"), ("QAW", 96 * k), 128, True, k > 0)
                mm("PV3", K("q1_%d" % k), ("QAW", 96 * k), 128, k == 0, False)
            mm("PV0", K("q3"), ("QRF", 0), 128, False, True)
            mm("PV3", K("q1_0"), ("QRF", 0), 128, False, True)
        ts(r("G3"), r("PA", 0, 96), 6.0, OP.mult, -3.0, OP.add)
        ts(r("G9"), r("PA", 0, 96), 9.0, OP.mult, 0.5, OP.add)

        def list1():
            tt(r("SB2"), r("PB", 0, C), r("MD"), OP.mult)
            scan(r("ST2"), r("ND"), r("SB2"))
            ts(r("PLo"), r("ST2", 15, C, 16), -1.0, OP.add)
            o = r("PLo")
            do("V", lambda e: e.tensor_copy(T.LW[:, 0:C].indirect(ap(o)), ap(r("IJF"))), [r("IJF"), o], [r("LW")])

        def list2():
            tt(r("SB3"), r("LW", 0, GW), r("MD", 0, GW), OP.mult)
            scan(r("ST3"), r("ND", 0, GW), r("SB3"))
            ts(r("ELo"), r("ST3", 15, GW, 16), P("A384"), OP.add)

        def gates():
            for b in range(4):
                act(r("E%d" % t, b, 4 * GW, 4), r("FT", 1536 * b, 1536 * b + 1536), scale=2.0, off=r("ELo"))

        def pass_on():
            quant("QE", 128 * t, 128 * t + 128, r("E%d" % t))
            send(t)

        def scores_at(k):
            return lambda: act(r("NB", C * k, C * k + C), r("TS"), off=r("OFT", 24 * k, 24 * k + 24))

        def order(j):
            a, b = ((0, 1), (0, 2), (1, 2))[j]
            return lambda: tt(r("RF", C * j, C * j + C), r("TS"), r("NB", C * a, C * a + C), OP.is_lt, off=r("OFT", 24 * b, 24 * b + 24))

        def orders():
            order(2)()
            quant("QRF", 0, 320, r("RF"))
            for j, (bk, a, ka, b, kb) in enumerate((("PA", 0, "qneg", 1, "qneg"), ("PB", 0, "qsel", 2, "qneg"))):
                mm(bk, K(ka), ("QRF", 96 * a), 128, True, False)
                mm(bk, K(kb), ("QRF", 96 * b), 128, False, True)

        def orders2():
            for j, bk in enumerate(("PA", "PB")): act(r("R%d" % j), r(bk, 0, 96), bias=3.0 - j)
            mm("PA", K("qsel"), ("QRF", 96), 128, True, False)
            mm("PA", K("qsel"), ("QRF", 192), 128, False, True)
            act(r("R2"), r("PA", 0, 96), bias=1.0)

        sq = [(A, j) for A in range(4) for j in range(7)]
        pend = []

        def slots(n):
            for _ in range(n):
                if not sq: return
                A, j = sq.pop(0)
                mm("PCC" if A % 2 == 0 else "PD", K("cls%d" % A), ("QT", C * (6 if j == 0 else j - 1)), C, j == 0, j == 6)
                if j == 6: pend.append(A)

        def slot_copies():
            while pend:
                A = pend.pop(0)
                act(r("SL", C * A, C * A + C), r("PCC" if A % 2 == 0 else "PD", 0, C), bias=float(C * A - 1))

        onS = [[scores_at(0)], [scores_at(1)], [gates], [], [], [orders2]]
        onV = [[list1], [list2], [order(0)], [pass_on, order(1)], [orders], []]
        if t == 0:
            setup_classes()
            for k in range(3): onS[k].append(lambda k=k: setup_hops(k))
            onS[3].append(setup_tables)
            for k in range(3):
                onS[1 + k].append(lambda k=k: setup_ends_s(k))
                onS[2 + k].append(lambda k=k: setup_ends(k))
            onV[0].append(lambda: quant_tiles("cls0", "cls3"))
            onV[0].append(setup_routes)
            onV[3].append(lambda: quant_tiles("hop0", "hop2"))
            onV[4].append(lambda: quant_tiles("hopf0", "gb"))
            onV[5].append(setup_layer)
        for i in range(SWEEPS):
            tt(r("MA"), r("PV0", 0, 96), r("G3"), OP.max)
            tt(r("MB"), r("PV1", 0, 96), r("MA"), OP.max)
            tt(r("MC"), r("PV2", 0, 96), r("MB"), OP.max)
            tt(r("TU"), r("PV3", 0, 96), r("MC"), OP.is_ge)
            if t == 0 or i: state()
            masked(r("TU"))
            ts(r("IN", 0, 4 * 96, 4), r("MC"), -1.0 / 3.0, OP.mult, 1.0, OP.add)
            quant("QIN", 0, 128, r("IN"))
            gather_w(VSWEEP[i])
            slot_copies()
            for f in onS[i]: f()
            inject(False)
            for f in onV[i]: f()
            quant("QGA", 0, 288, r("GA", 0, 1152))
            for k in range(3): mm("PV%d" % k, K("came%d" % k), ("QGA", 96 * k), 128, False, True)
            for k in range(3): mm("PV3", K("own%d" % k), ("QGA", 96 * k), 128, False, k == 2)
            slots(SLOTS[i])
        for k in range(3): tt(r("va%d" % k), r("PV%d" % k, 0, 96), r("R%d" % k), OP.min)
        if t < R - 1:
            state()
            act(r("IN", 0, 4 * 96, 4), r("PV0", 0, 96), scale=0.0)
        else:
            ts(r("ba"), r("PV3", 0, 96), 1.0, OP.is_ge, P("bit"), OP.mult)
            ts(r("bb"), r("PV3", 0, 96), -1.0, OP.is_le, P("bit8"), OP.mult)
        for k in range(3): tt(r("mx%d" % k), r("va%d" % k), r("G9") if k == 0 else r("mx%d" % (k - 1)), OP.max)
        for k in range(3): tt(r("pk%d" % k), r("va%d" % k), r("mx2"), OP.is_ge)
        tt(r("self"), r("mx2"), r("G9"), OP.is_equal)
        tt(r("SJ"), r("self"), r("JC"), OP.mult)
        for k in range(3): tt(r("t%d" % k), r("pk%d" % k), r("OC%d" % k), OP.mult)
        tt(r("ua"), r("t0"), r("SJ"), OP.add)
        tt(r("ub"), r("t1"), r("t2"), OP.add)
        tt(r("PP"), r("ua"), r("ub"), OP.add)
        masked(r("PP"))
        gather_w(VHOP)
        slot_copies()
        quant("QW", 0, 128, r("W"))
        mm("PV3", K("hopf0"), ("QW", 0), 128)
        quant("QGA", 0, 288, r("GA", 0, 1152))
        for k in range(3): mm("PV%d" % k, K("hop%d" % k), ("QGA", 96 * k), 128)
        slots(SLOTS[SWEEPS])
        to_list(r("PV3", 0, 96), r("DL"))
        for k in range(3): tt(r("t%d" % k), r("PV%d" % k, 0, 96), r("pk%d" % k), OP.mult)
        tt(r("ua"), r("t0"), r("SJ"), OP.add)
        tt(r("ub"), r("t1"), r("t2"), OP.add)
        tt(r("PP"), r("ua"), r("ub"), OP.add)
        masked(r("PP"))
        quant("QW", 0, 128, r("W"))
        mm("PV2", K("ct2"), ("QW", 0), 128)
        mm("PV0", K("ct0"), ("QW", 0), 128)
        mm("PA", K("hopf0"), ("QW", 0), 128)
        mm("PV1", K("ct1"), ("QW", 0), 128)
        mm("PV3", K("ct3"), ("QW", 0), 128)
        slot_copies()
        for A in (2, 3, 0, 1):
            for s in range(4):
                o, x = r("WA", C * A + s, C * A + C, 4), r("PV%d" % A, 0, 96)
                if A < 2: ts(o, x, P("ms%d" % s), OP.mult)
                else: act(o, x, scale=P("ms%d" % s))
        to_list(r("PA", 0, 96), r("EL"))
        act(r("GA", 192, C), r("WA"), off=r("EL", 12, 24))
        tc(r("GA", 0, 192), r("WA"), off=r("EL", 0, 12))
        for b in range(4):
            act(r("FD", C * b, C * b + C), r("FT", 1536 * b, 1536 * b + 1536), off=r("DL"))
        quant("QG", 0, 128, r("GA", 0, 512))
        mm("PB", K("hopf0"), ("QG", 0), 128)
        a, o = (0, 0) if t == 0 else (GW * t, 32)
        for j in range(8):
            two = [("PV0", "PV1", "PV2", "PV3")[2 * (j % 2) + i] for i in range(2)]
            for i in range(2): mm(two[i], ("WP", 256 * j + 128 * i), ("LD", a), 128)
            for i in range(2):
                b, A = j // 2, 2 * (j % 2) + i
                act(r("HT", 1536 * b + C * A, 1536 * b + C * A + GW), r(two[i], o, o + GW), scale=0.015625)
        to_list(r("PB", 0, 96), r("EL"))
        if t == R - 1:
            tc(r("PE"), r("PB", 0, 96))
            number_parts()
        tt(r("SB2"), r("SL"), r("MD"), OP.mult, off=r("EL"))
        scan(r("ST2"), r("ND"), r("SB2"))
        tc(r("HL"), r("ST2", 15, C, 16))
        for b in range(4):
            tt(r("Z", C * b, C * b + C), r("FT", 1536 * b, 1536 * b + 1536), r("FD", C * b, C * b + C), OP.add, off=r("EL"))
        for b in range(4):
            tt(r("X0", b, 4 * C, 4), r("HT", 1536 * b, 1536 * b + 1536), r("Z", C * b, C * b + C), OP.add, off=r("HL"))
        quant("QX", 0, C, r("X0"))
        if t == 0: quant("QV", 0, 128, r("VV"))
    mm("PA", ("QV", 0), ("QX", 0), C)
    act(r("TS", 2 * C, 3 * C), r("PA", 0, C))
    dma("Y", "d7", [(T.oc[:], T.QXc[:, 0:C].bitcast(dt.uint8))] + [(T.osc[4 * k:4 * k + 4, :], T.QXs[32 * k:32 * k + 4, 0:C]) for k in range(4)], rd=[r("QXc"), r("QXs")])
    dma("Y", "d8", [(T.y[:], T.TS[:, 2 * C:3 * C])], rd=[r("TS", 2 * C, 3 * C)])
    quant("QND", 0, C, r("ET"))
    mm("PB", K("ge"), ("QND", 0), C, True, False)
    mm("PB", K("gm"), ("QND", 0), C, False, True)
    mm("PCC", K("gb"), ("QND", 0), C)
    act(r("TS", 0, C), r("PB", 0, C))
    act(r("TS", C, 2 * C), r("PCC", 0, C))
    dma("Y", "d9", [(T.nd[:], T.TS[0:128:16, 0:2 * C])], rd=[r("TS", 0, 2 * C)])
    for s in SEMAPHORES:
        if cnt[s]: g.wait_ge(T.sem[s], cnt[s])
